import numpy as np
import ml_dtypes


def mxq(x, axis, fmt="e4m3"):
    dtype, down = {"e4m3": (ml_dtypes.float8_e4m3fn, 7), "e5m2": (ml_dtypes.float8_e5m2, 14)}[fmt]
    v = np.moveaxis(np.asarray(x, np.float32).astype(ml_dtypes.bfloat16).astype(np.float64), axis, -1)
    blocks = v.reshape(v.shape[:-1] + (-1, 32))
    amax = np.abs(blocks).max(-1, keepdims=True)
    byte = np.maximum(np.where(amax > 0, np.frexp(amax)[1] - 1 + 127, 0) - down, 1)
    scale = np.exp2(byte - 127.0)
    codes = (blocks / scale).astype(np.float32).astype(dtype).astype(np.float64)
    return np.moveaxis((codes * scale).reshape(v.shape), -1, axis)


WIDE = False


def mx_kscale(k):
    if not WIDE:
        return np.ones(k)
    levels = np.array([10, -10, 5, -5, 0])
    if k % 512:
        return np.exp2(np.random.permutation(np.resize(levels, k // 32))).repeat(32)
    a = np.empty((k // 512, 16))
    for p in range(k // 512):
        a[p, :8] = np.random.permutation(np.resize(levels, 8))
        for g in range(8):
            far = levels[np.abs(levels - a[p, g]) >= 10]
            a[p, g + 8] = far[np.random.randint(len(far))]
    return np.exp2(a.ravel()).repeat(32)


def f64(x):
    return np.asarray(x).astype(np.float64)


def striped(idx):
    return np.tile(idx.reshape(-1, 16).T, (8, 1)).astype(np.uint16)


def unstriped(offs):
    return offs[:16].T.reshape(-1).astype(np.int64)


def pack_weight(w):
    k, n = w.shape
    w = f64(np.asarray(w, np.float32).astype(ml_dtypes.bfloat16)).reshape(k // 32, 32, n)
    amax = np.abs(w).max(1)
    byte = np.clip(np.where(amax > 0, np.frexp(amax)[1] - 1 + 127 - 7, 1), 1, 254)
    scaled = (w * np.exp2(127.0 - byte)[:, None, :]).reshape(k, n).astype(np.float32)
    words = np.ascontiguousarray(scaled.reshape(k // 512, 128, 4, n).transpose(0, 1, 3, 2)).astype(ml_dtypes.float8_e4m3fn).view(np.uint8)
    return words, np.ascontiguousarray(byte.astype(np.uint8).reshape(k // 512, 16, n))


def unpack_weight(words, scales):
    g, p, n, _ = words.shape
    vals = np.ascontiguousarray(words).view(ml_dtypes.float8_e4m3fn).astype(np.float64) * np.repeat(np.exp2(scales.astype(np.float64) - 127.0), 8, axis=1)[..., None]
    return vals.transpose(0, 1, 3, 2).reshape(g * 512, n)


K, T, S, V, N = 1024, 1024, 512, 256, 256
P = 2 ** 7


def setup_inputs():
    n = np.random.standard_normal
    s = mx_kscale(K)[:, None]
    packed_w1 = pack_weight(n((K, N)) / np.sqrt(K) / s)
    return {
        "xT": (n((K, T)) * s).astype(np.float32),
        "w1_words": packed_w1[0],
        "w1_scales": packed_w1[1],
        "frac": np.tile(np.random.uniform(0.05, 0.95, V), (P, 1)).astype(np.float32),
        "offs": striped(np.random.permutation(T)[:S]),
        "left": striped(np.random.permutation(S)[:V]),
        "right": striped(np.random.permutation(S)[:V]),
    }


def reference(xT, w1_words, w1_scales, frac, offs, left, right):
    xq = mxq(f64(xT)[:, unstriped(offs)], 0, "e4m3")
    y = unpack_weight(w1_words, w1_scales).T @ xq
    l = y[:, unstriped(left)]
    return l + (y[:, unstriped(right)] - l) * f64(frac)[:1]

@@ -1,0 +1,149 @@
+from contextlib import ExitStack
+
+import concourse.mybir as mybir
+
+K, T, S, V, N = 1024, 1024, 512, 256, 256
+FLOPS = 2 * K * S * N
+
+F32 = mybir.dt.float32
+BF16 = mybir.dt.bfloat16
+I32 = mybir.dt.int32
+U32 = mybir.dt.uint32
+U16 = mybir.dt.uint16
+U8 = mybir.dt.uint8
+FP8X4 = mybir.dt.float8_e4m3fn_x4
+MULT = mybir.AluOpType.mult
+ADD = mybir.AluOpType.add
+
+P = 128
+PASSES = 2
+FIRST_SLICES = (256, 256)
+LAST_SLICES = (128, 128, 128, 128)
+
+
+def bounds(widths):
+    edges = [0]
+    for w in widths:
+        edges.append(edges[-1] + w)
+    return list(zip(edges[:-1], edges[1:]))
+
+
+def tile_picked_lerp_none_e_kernel(tc, xT, w1_words, w1_scales, frac, offs, left, right, out):
+    nc = tc.nc
+    with ExitStack() as ctx:
+        lists = ctx.enter_context(tc.tile_pool(name="lists", bufs=1))
+        sb = ctx.enter_context(tc.tile_pool(name="sb", bufs=1))
+        psum = ctx.enter_context(tc.psum_pool(name="psum", bufs=1))
+
+        offs_sb = lists.tile([P, S // 16], U16, name="offs_sb")
+        left_sb = lists.tile([P, V // 16], U16, name="left_sb")
+        right_sb = lists.tile([P, V // 16], U16, name="right_sb")
+
+        x_rows = xT.rearrange("(g p u e) t -> g u p e t", g=PASSES, u=2, e=2)
+        raw = {}
+        pairs = {}
+        for g in range(PASSES):
+            for u in range(2):
+                raw[g, u] = sb.tile([P, 2, T], F32, name="raw%d%d" % (g, u))
+                pairs[g, u] = sb.tile([P, 2 * T], BF16, name="pairs%d%d" % (g, u), align_bytes=64)
+        w_words = sb.tile([P, PASSES, N], U32, name="w_words", align_bytes=64)
+        w_scales = sb.tile([P, PASSES, N], U8, name="w_scales", align_bytes=64)
+        f_right = sb.tile([P, V], F32, name="f_right")
+        f_left = sb.tile([P, V], F32, name="f_left")
+
+        nc.sync.dma_start(raw[0, 0][:], x_rows[0, 0])
+        nc.sync.dma_start(offs_sb[:], offs)
+        nc.sync.dma_start(raw[0, 1][:], x_rows[0, 1])
+        nc.sync.dma_start(raw[1, 0][:], x_rows[1, 0])
+        nc.sync.dma_start(raw[1, 1][:, 0, :], x_rows[1, 1][:, 0, :])
+        nc.sync.dma_start(raw[1, 1][:, 1, 0:512], x_rows[1, 1][:, 1, 0:512])
+        nc.sync.dma_start(raw[1, 1][:, 1, 512:1024], x_rows[1, 1][:, 1, 512:1024])
+        nc.gpsimd.memset(w_scales[:].rearrange("p g n -> p (g n)").bitcast(I32), 0)
+        for q in range(4):
+            nc.sync.dma_start(
+                w_scales[32 * q : 32 * q + 4, :, :].bitcast(I32),
+                w1_scales[:, 4 * q : 4 * q + 4, :].rearrange("g r n -> r g n").bitcast(I32),
+            )
+        nc.sync.dma_start(w_words[:].bitcast(I32), w1_words.rearrange("g p n t -> p g (n t)").bitcast(I32))
+        nc.sync.dma_start(f_right[:], frac)
+        nc.sync.dma_start(right_sb[:], right)
+        nc.sync.dma_start(left_sb[:], left)
+
+        def cast(g, u, a, b, split):
+            src = raw[g, u]
+            dst = pairs[g, u][:].rearrange("p (t e) -> p t e", e=2)
+            nc.scalar.copy(dst[:, a:split, :], src[:, :, a:split].rearrange("p e t -> p t e"))
+            nc.vector.tensor_copy(dst[:, split:b, :], src[:, :, split:b].rearrange("p e t -> p t e"))
+
+        picked = [sb.tile([P, 2, S], U32, name="picked%d" % g) for g in range(PASSES)]
+
+        def gather(dst, g, u, a, b):
+            nc.vector.tensor_copy(dst, pairs[g, u][:].bitcast(U32).indirect(offs_sb[:, a // 16 : b // 16]))
+
+        codes = [sb.tile([P, S], U32, name="codes%d" % g, align_bytes=64) for g in range(PASSES)]
+        scales = [sb.tile([P, S], U8, name="scales%d" % g, align_bytes=64) for g in range(PASSES)]
+
+        def weave(g, i, a, b):
+            woven = sb.tile([P, 4 * (b - a)], BF16, name="woven%d%d" % (g, i), align_bytes=64)
+            nc.scalar.copy(woven[:].bitcast(U32).rearrange("p (s u) -> p s u", u=2), picked[g][:, :, a:b].rearrange("p u s -> p s u"))
+            return woven
+
+        def quantize(g, woven, a, b):
+            nc.vector.quantize_mx(out=codes[g][:, a:b].bitcast(FP8X4), scales=scales[g][:, a:b], in_=woven[:])
+
+        cast(0, 0, 0, T, 352)
+        gather(picked[0][:, 0, :], 0, 0, 0, S)
+        cast(0, 1, 0, T, 384)
+        woven = {}
+        for i, (a, b) in enumerate(bounds(FIRST_SLICES)):
+            gather(picked[0][:, 1, a:b], 0, 1, a, b)
+            woven[0, i] = weave(0, i, a, b)
+        quantize(0, woven[0, 0], 0, 256)
+        cast(1, 0, 0, T, 352)
+        quantize(0, woven[0, 1], 256, 512)
+        gather(picked[1][:, 0, :], 1, 0, 0, S)
+        cast(1, 1, 0, 512, 448)
+        cast(1, 1, 512, 1024, 640)
+
+        banks = {}
+        for m, widths in ((0, LAST_SLICES), (1, FIRST_SLICES)):
+            for i, w in enumerate(widths):
+                banks[m, i] = psum.tile([P, w], F32, name="bank%d%d" % (m, i))
+
+        def product(m, i, g, a, b):
+            cols = slice(m * P, (m + 1) * P)
+            nc.tensor.matmul_mx(
+                out=banks[m, i][:],
+                lhsT=w_words[:, g, cols].bitcast(FP8X4),
+                lhsT_scale=w_scales[:, g, cols],
+                rhs=codes[g][:, a:b].bitcast(FP8X4),
+                rhs_scale=scales[g][:, a:b],
+                start=(g == 0),
+                stop=(g == PASSES - 1),
+            )
+
+        y = [sb.tile([P, S], F32, name="y%d" % m) for m in range(2)]
+        for i, (a, b) in enumerate(bounds(LAST_SLICES)):
+            product(0, i, 0, a, b)
+        for i, (a, b) in enumerate(bounds(LAST_SLICES)):
+            gather(picked[1][:, 1, a:b], 1, 1, a, b)
+            woven[1, i] = weave(1, i, a, b)
+        for i, (a, b) in enumerate(bounds(LAST_SLICES)):
+            quantize(1, woven[1, i], a, b)
+            product(0, i, 1, a, b)
+            nc.scalar.copy(y[0][:, a:b], banks[0, i][:])
+        for i, (a, b) in enumerate(bounds(FIRST_SLICES)):
+            product(1, i, 0, a, b)
+        for i, (a, b) in enumerate(bounds(FIRST_SLICES)):
+            product(1, i, 1, a, b)
+            nc.scalar.copy(y[1][:, a:b], banks[1, i][:])
+
+        nc.vector.tensor_scalar(f_left[:], f_right[:], -1.0, 1.0, MULT, ADD)
+        for m in range(2):
+            lo = sb.tile([P, V], F32, name="lo%d" % m)
+            hi = sb.tile([P, V], F32, name="hi%d" % m)
+            res = sb.tile([P, V], F32, name="res%d" % m)
+            nc.vector.tensor_tensor(hi[:], y[m][:].indirect(right_sb[:]), f_right[:], MULT)
+            nc.vector.tensor_tensor(lo[:], y[m][:].indirect(left_sb[:]), f_left[:], MULT)
+            nc.vector.tensor_tensor(res[:], lo[:], hi[:], ADD)
+            nc.sync.dma_start(out[m * P : (m + 1) * P, :], res[:])

@@ -17,15 +17,16 @@ ADD = mybir.AluOpType.add
 
 P = 128
 PASSES = 2
-FIRST_SLICES = (256, 256)
-LAST_SLICES = (128, 128, 128, 128)
-
-
-def bounds(widths):
-    edges = [0]
-    for w in widths:
-        edges.append(edges[-1] + w)
-    return list(zip(edges[:-1], edges[1:]))
+LAST_SLICES = ((0, 256), (256, 384), (384, 512))
+CHUNKS = (
+    (0, 0, 0, 1024, 400),
+    (0, 1, 0, 512, 512),
+    (0, 1, 512, 1024, 200),
+    (1, 0, 0, 512, 304),
+    (1, 0, 512, 1024, 0),
+    (1, 1, 0, 512, 512),
+    (1, 1, 512, 1024, 280),
+)
 
 
 def tile_picked_lerp_none_e_kernel(tc, xT, w1_words, w1_scales, frac, offs, left, right, out):
@@ -40,24 +41,21 @@ def tile_picked_lerp_none_e_kernel(tc, xT, w1_words, w1_scales, frac, offs, left
         right_sb = lists.tile([P, V // 16], U16, name="right_sb")
 
         x_rows = xT.rearrange("(g p u e) t -> g u p e t", g=PASSES, u=2, e=2)
-        raw = {}
         pairs = {}
         for g in range(PASSES):
             for u in range(2):
-                raw[g, u] = sb.tile([P, 2, T], F32, name="raw%d%d" % (g, u))
                 pairs[g, u] = sb.tile([P, 2 * T], BF16, name="pairs%d%d" % (g, u), align_bytes=64)
         w_words = sb.tile([P, PASSES, N], U32, name="w_words", align_bytes=64)
         w_scales = sb.tile([P, PASSES, N], U8, name="w_scales", align_bytes=64)
         f_right = sb.tile([P, V], F32, name="f_right")
-        f_left = sb.tile([P, V], F32, name="f_left")
 
-        nc.sync.dma_start(raw[0, 0][:], x_rows[0, 0])
-        nc.sync.dma_start(offs_sb[:], offs)
-        nc.sync.dma_start(raw[0, 1][:], x_rows[0, 1])
-        nc.sync.dma_start(raw[1, 0][:], x_rows[1, 0])
-        nc.sync.dma_start(raw[1, 1][:, 0, :], x_rows[1, 1][:, 0, :])
-        nc.sync.dma_start(raw[1, 1][:, 1, 0:512], x_rows[1, 1][:, 1, 0:512])
-        nc.sync.dma_start(raw[1, 1][:, 1, 512:1024], x_rows[1, 1][:, 1, 512:1024])
+        raw = []
+        for c, (g, u, a, b, share) in enumerate(CHUNKS):
+            raw.append(sb.tile([P, 2, b - a], F32, name="raw%d" % c, tag="raw%d" % c, align_bytes=64))
+            nc.sync.dma_start(raw[c][:], x_rows[g, u][:, :, a:b])
+            if c == 0:
+                nc.sync.dma_start(offs_sb[:], offs)
+
         nc.gpsimd.memset(w_scales[:].rearrange("p g n -> p (g n)").bitcast(I32), 0)
         for q in range(4):
             nc.sync.dma_start(
@@ -69,51 +67,56 @@ def tile_picked_lerp_none_e_kernel(tc, xT, w1_words, w1_scales, frac, offs, left
         nc.sync.dma_start(right_sb[:], right)
         nc.sync.dma_start(left_sb[:], left)
 
-        def cast(g, u, a, b, split):
-            src = raw[g, u]
+        def cast(c):
+            g, u, a, b, share = CHUNKS[c]
+            src = raw[c][:].rearrange("p e t -> p t e")
             dst = pairs[g, u][:].rearrange("p (t e) -> p t e", e=2)
-            nc.scalar.copy(dst[:, a:split, :], src[:, :, a:split].rearrange("p e t -> p t e"))
-            nc.vector.tensor_copy(dst[:, split:b, :], src[:, :, split:b].rearrange("p e t -> p t e"))
+            if share > 0:
+                nc.scalar.copy(dst[:, a : a + share, :], src[:, 0:share, :])
+            if a + share < b:
+                nc.vector.tensor_copy(dst[:, a + share : b, :], src[:, share : b - a, :])
+
+        def cast_pair(g, u):
+            for c, chunk in enumerate(CHUNKS):
+                if chunk[0] == g and chunk[1] == u:
+                    cast(c)
 
         picked = [sb.tile([P, 2, S], U32, name="picked%d" % g) for g in range(PASSES)]
 
-        def gather(dst, g, u, a, b):
-            nc.vector.tensor_copy(dst, pairs[g, u][:].bitcast(U32).indirect(offs_sb[:, a // 16 : b // 16]))
+        def gather(g, u, a, b):
+            nc.vector.tensor_copy(picked[g][:, u, a:b], pairs[g, u][:].bitcast(U32).indirect(offs_sb[:, a // 16 : b // 16]))
 
         codes = [sb.tile([P, S], U32, name="codes%d" % g, align_bytes=64) for g in range(PASSES)]
         scales = [sb.tile([P, S], U8, name="scales%d" % g, align_bytes=64) for g in range(PASSES)]
 
-        def weave(g, i, a, b):
-            woven = sb.tile([P, 4 * (b - a)], BF16, name="woven%d%d" % (g, i), align_bytes=64)
+        def weave(g, a, b, tag):
+            woven = sb.tile([P, 4 * (b - a)], BF16, name="woven%d_%d" % (g, a), tag=tag, align_bytes=64)
             nc.scalar.copy(woven[:].bitcast(U32).rearrange("p (s u) -> p s u", u=2), picked[g][:, :, a:b].rearrange("p u s -> p s u"))
             return woven
 
         def quantize(g, woven, a, b):
             nc.vector.quantize_mx(out=codes[g][:, a:b].bitcast(FP8X4), scales=scales[g][:, a:b], in_=woven[:])
 
-        cast(0, 0, 0, T, 352)
-        gather(picked[0][:, 0, :], 0, 0, 0, S)
-        cast(0, 1, 0, T, 384)
         woven = {}
-        for i, (a, b) in enumerate(bounds(FIRST_SLICES)):
-            gather(picked[0][:, 1, a:b], 0, 1, a, b)
-            woven[0, i] = weave(0, i, a, b)
-        quantize(0, woven[0, 0], 0, 256)
-        cast(1, 0, 0, T, 352)
-        quantize(0, woven[0, 1], 256, 512)
-        gather(picked[1][:, 0, :], 1, 0, 0, S)
-        cast(1, 1, 0, 512, 448)
-        cast(1, 1, 512, 1024, 640)
+        cast_pair(0, 0)
+        gather(0, 0, 0, S)
+        cast_pair(0, 1)
+        gather(0, 1, 0, S)
+        cast_pair(1, 0)
+        woven[0, 0] = weave(0, 0, S, "raw3")
+        gather(1, 0, 0, S)
+        quantize(0, woven[0, 0], 0, S)
+        cast_pair(1, 1)
 
         banks = {}
-        for m, widths in ((0, LAST_SLICES), (1, FIRST_SLICES)):
-            for i, w in enumerate(widths):
-                banks[m, i] = psum.tile([P, w], F32, name="bank%d%d" % (m, i))
+        for a, b in LAST_SLICES:
+            banks[0, a] = psum.tile([P, b - a], F32, name="bank0_%d" % a)
+        banks[1, 0] = psum.tile([P, S], F32, name="bank1")
 
-        def product(m, i, g, a, b):
+        def product(m, g, a, b):
             cols = slice(m * P, (m + 1) * P)
             nc.tensor.matmul_mx(
-                out=banks[m, i][:],
+                out=banks[m, a][:],
                 lhsT=w_words[:, g, cols].bitcast(FP8X4),
                 lhsT_scale=w_scales[:, g, cols],
                 rhs=codes[g][:, a:b].bitcast(FP8X4),
@@ -123,21 +126,20 @@ def tile_picked_lerp_none_e_kernel(tc, xT, w1_words, w1_scales, frac, offs, left
             )
 
         y = [sb.tile([P, S], F32, name="y%d" % m) for m in range(2)]
-        for i, (a, b) in enumerate(bounds(LAST_SLICES)):
-            product(0, i, 0, a, b)
-        for i, (a, b) in enumerate(bounds(LAST_SLICES)):
-            gather(picked[1][:, 1, a:b], 1, 1, a, b)
-            woven[1, i] = weave(1, i, a, b)
-        for i, (a, b) in enumerate(bounds(LAST_SLICES)):
-            quantize(1, woven[1, i], a, b)
-            product(0, i, 1, a, b)
-            nc.scalar.copy(y[0][:, a:b], banks[0, i][:])
-        for i, (a, b) in enumerate(bounds(FIRST_SLICES)):
-            product(1, i, 0, a, b)
-        for i, (a, b) in enumerate(bounds(FIRST_SLICES)):
-            product(1, i, 1, a, b)
-            nc.scalar.copy(y[1][:, a:b], banks[1, i][:])
+        for a, b in LAST_SLICES:
+            product(0, 0, a, b)
+        product(1, 0, 0, S)
+        for a, b in LAST_SLICES:
+            gather(1, 1, a, b)
+            woven[1, a] = weave(1, a, b, "woven%d" % a)
+        for a, b in LAST_SLICES:
+            quantize(1, woven[1, a], a, b)
+            product(0, 1, a, b)
+            nc.scalar.copy(y[0][:, a:b], banks[0, a][:])
+        product(1, 1, 0, S)
+        nc.scalar.copy(y[1][:], banks[1, 0][:])
 
+        f_left = sb.tile([P, V], F32, name="f_left", tag="woven384", align_bytes=64)
         nc.vector.tensor_scalar(f_left[:], f_right[:], -1.0, 1.0, MULT, ADD)
         for m in range(2):
             lo = sb.tile([P, V], F32, name="lo%d" % m)

@@ -17,15 +17,16 @@ ADD = mybir.AluOpType.add
 
 P = 128
 PASSES = 2
-LAST_SLICES = ((0, 256), (256, 384), (384, 512))
+FIRST_SLICES = ((0, 256), (256, 512))
+LAST_SLICES = ((0, 128), (128, 256), (256, 384), (384, 512))
 CHUNKS = (
     (0, 0, 0, 1024, 400),
     (0, 1, 0, 512, 512),
-    (0, 1, 512, 1024, 200),
-    (1, 0, 0, 512, 304),
-    (1, 0, 512, 1024, 0),
+    (0, 1, 512, 1024, 192),
+    (1, 0, 0, 512, 192),
+    (1, 0, 512, 1024, 192),
     (1, 1, 0, 512, 512),
-    (1, 1, 512, 1024, 280),
+    (1, 1, 512, 1024, 224),
 )
 
 
@@ -76,15 +77,10 @@ def tile_picked_lerp_none_e_kernel(tc, xT, w1_words, w1_scales, frac, offs, left
             if a + share < b:
                 nc.vector.tensor_copy(dst[:, a + share : b, :], src[:, share : b - a, :])
 
-        def cast_pair(g, u):
-            for c, chunk in enumerate(CHUNKS):
-                if chunk[0] == g and chunk[1] == u:
-                    cast(c)
-
         picked = [sb.tile([P, 2, S], U32, name="picked%d" % g) for g in range(PASSES)]
 
-        def gather(g, u, a, b):
-            nc.vector.tensor_copy(picked[g][:, u, a:b], pairs[g, u][:].bitcast(U32).indirect(offs_sb[:, a // 16 : b // 16]))
+        def gather(dst, g, u, a, b):
+            nc.vector.tensor_copy(dst, pairs[g, u][:].bitcast(U32).indirect(offs_sb[:, a // 16 : b // 16]))
 
         codes = [sb.tile([P, S], U32, name="codes%d" % g, align_bytes=64) for g in range(PASSES)]
         scales = [sb.tile([P, S], U8, name="scales%d" % g, align_bytes=64) for g in range(PASSES)]
@@ -98,15 +94,19 @@ def tile_picked_lerp_none_e_kernel(tc, xT, w1_words, w1_scales, frac, offs, left
             nc.vector.quantize_mx(out=codes[g][:, a:b].bitcast(FP8X4), scales=scales[g][:, a:b], in_=woven[:])
 
         woven = {}
-        cast_pair(0, 0)
-        gather(0, 0, 0, S)
-        cast_pair(0, 1)
-        gather(0, 1, 0, S)
-        cast_pair(1, 0)
-        woven[0, 0] = weave(0, 0, S, "raw3")
-        gather(1, 0, 0, S)
-        quantize(0, woven[0, 0], 0, S)
-        cast_pair(1, 1)
+        cast(0)
+        gather(picked[0][:, 0, :], 0, 0, 0, S)
+        cast(1)
+        cast(2)
+        for a, b in FIRST_SLICES:
+            gather(picked[0][:, 1, a:b], 0, 1, a, b)
+        for i, (a, b) in enumerate(FIRST_SLICES):
+            woven[0, a] = weave(0, a, b, "first%d" % a)
+            cast(3 + i)
+            quantize(0, woven[0, a], a, b)
+        gather(picked[1][:, 0, :], 1, 0, 0, S)
+        cast(5)
+        cast(6)
 
         banks = {}
         for a, b in LAST_SLICES:
@@ -130,7 +130,7 @@ def tile_picked_lerp_none_e_kernel(tc, xT, w1_words, w1_scales, frac, offs, left
             product(0, 0, a, b)
         product(1, 0, 0, S)
         for a, b in LAST_SLICES:
-            gather(1, 1, a, b)
+            gather(picked[1][:, 1, a:b], 1, 1, a, b)
             woven[1, a] = weave(1, a, b, "woven%d" % a)
         for a, b in LAST_SLICES:
             quantize(1, woven[1, a], a, b)
@@ -141,11 +141,12 @@ def tile_picked_lerp_none_e_kernel(tc, xT, w1_words, w1_scales, frac, offs, left
 
         f_left = sb.tile([P, V], F32, name="f_left", tag="woven384", align_bytes=64)
         nc.vector.tensor_scalar(f_left[:], f_right[:], -1.0, 1.0, MULT, ADD)
+        lo = [sb.tile([P, V], F32, name="lo%d" % m) for m in range(2)]
+        hi = [sb.tile([P, V], F32, name="hi%d" % m) for m in range(2)]
         for m in range(2):
-            lo = sb.tile([P, V], F32, name="lo%d" % m)
-            hi = sb.tile([P, V], F32, name="hi%d" % m)
-            res = sb.tile([P, V], F32, name="res%d" % m)
-            nc.vector.tensor_tensor(hi[:], y[m][:].indirect(right_sb[:]), f_right[:], MULT)
-            nc.vector.tensor_tensor(lo[:], y[m][:].indirect(left_sb[:]), f_left[:], MULT)
-            nc.vector.tensor_tensor(res[:], lo[:], hi[:], ADD)
+            nc.vector.tensor_tensor(hi[m][:], y[m][:].indirect(right_sb[:]), f_right[:], MULT)
+            nc.vector.tensor_tensor(lo[m][:], y[m][:].indirect(left_sb[:]), f_left[:], MULT)
+        for m in range(2):
+            res = sb.tile([P, V], F32, name="res%d" % m, tag=("woven384", "res1")[m], align_bytes=64)
+            nc.vector.tensor_tensor(res[:], lo[m][:], hi[m][:], ADD)
             nc.sync.dma_start(out[m * P : (m + 1) * P, :], res[:])

@@ -17,17 +17,20 @@ ADD = mybir.AluOpType.add
 
 P = 128
 PASSES = 2
-FIRST_SLICES = ((0, 256), (256, 512))
-LAST_SLICES = ((0, 128), (128, 256), (256, 384), (384, 512))
-CHUNKS = (
-    (0, 0, 0, 1024, 400),
-    (0, 1, 0, 512, 512),
-    (0, 1, 512, 1024, 192),
-    (1, 0, 0, 512, 192),
-    (1, 0, 512, 1024, 192),
-    (1, 1, 0, 512, 512),
-    (1, 1, 512, 1024, 224),
+LOADS = (
+    (0, "run", 0, 1536),
+    (0, "run", 1536, 2048),
+    (1, "cols", 0, 512),
+    (1, "cols", 512, 1024),
+    (2, "cols", 0, 256),
+    (2, "cols", 256, 640),
+    (2, "cols", 640, 1024),
+    (3, "cols", 0, 384),
+    (3, "cols", 384, 768),
+    (3, "cols", 768, 1024),
 )
+LAST_SLICES = ((0, 128), (128, 256), (256, 384), (384, 512),)
+ROW1_SLICES = ((0, 512),)
 
 
 def tile_picked_lerp_none_e_kernel(tc, xT, w1_words, w1_scales, frac, offs, left, right, out):
@@ -41,19 +44,24 @@ def tile_picked_lerp_none_e_kernel(tc, xT, w1_words, w1_scales, frac, offs, left
         left_sb = lists.tile([P, V // 16], U16, name="left_sb")
         right_sb = lists.tile([P, V // 16], U16, name="right_sb")
 
+        x_runs = xT.rearrange("(g p u e) t -> g u p (e t)", g=PASSES, u=2, e=2)
         x_rows = xT.rearrange("(g p u e) t -> g u p e t", g=PASSES, u=2, e=2)
-        pairs = {}
-        for g in range(PASSES):
-            for u in range(2):
-                pairs[g, u] = sb.tile([P, 2 * T], BF16, name="pairs%d%d" % (g, u), align_bytes=64)
+        pairs = [sb.tile([P, 2 * T], BF16, name="pairs%d" % i, align_bytes=64) for i in range(4)]
         w_words = sb.tile([P, PASSES, N], U32, name="w_words", align_bytes=64)
         w_scales = sb.tile([P, PASSES, N], U8, name="w_scales", align_bytes=64)
         f_right = sb.tile([P, V], F32, name="f_right")
 
-        raw = []
-        for c, (g, u, a, b, share) in enumerate(CHUNKS):
-            raw.append(sb.tile([P, 2, b - a], F32, name="raw%d" % c, tag="raw%d" % c, align_bytes=64))
-            nc.sync.dma_start(raw[c][:], x_rows[g, u][:, :, a:b])
+        runs = {}
+        cols = []
+        for c, (i, kind, a, b) in enumerate(LOADS):
+            if kind == "run":
+                if i not in runs:
+                    runs[i] = sb.tile([P, 2 * T], F32, name="run%d" % i, align_bytes=64)
+                nc.sync.dma_start(runs[i][:, a:b], x_runs[i // 2, i % 2][:, a:b])
+            else:
+                piece = sb.tile([P, 2, b - a], F32, name="cols%d" % c, tag="cols%d" % c, align_bytes=64)
+                cols.append((i, a, b, piece))
+                nc.sync.dma_start(piece[:], x_rows[i // 2, i % 2][:, :, a:b])
             if c == 0:
                 nc.sync.dma_start(offs_sb[:], offs)
 
@@ -68,78 +76,107 @@ def tile_picked_lerp_none_e_kernel(tc, xT, w1_words, w1_scales, frac, offs, left
         nc.sync.dma_start(right_sb[:], right)
         nc.sync.dma_start(left_sb[:], left)
 
-        def cast(c):
-            g, u, a, b, share = CHUNKS[c]
-            src = raw[c][:].rearrange("p e t -> p t e")
-            dst = pairs[g, u][:].rearrange("p (t e) -> p t e", e=2)
-            if share > 0:
-                nc.scalar.copy(dst[:, a : a + share, :], src[:, 0:share, :])
-            if a + share < b:
-                nc.vector.tensor_copy(dst[:, a + share : b, :], src[:, share : b - a, :])
+        def cast(copy, i, a, b):
+            dst = pairs[i][:].rearrange("p (t e) -> p t e", e=2)[:, a:b, :]
+            if i in runs:
+                copy(dst, runs[i][:].rearrange("p (e t) -> p t e", e=2)[:, a:b, :])
+            else:
+                first, piece = [(lo, piece) for j, lo, hi, piece in cols if j == i and lo <= a and b <= hi][0]
+                copy(dst, piece[:].rearrange("p e t -> p t e")[:, a - first : b - first, :])
 
+        on_s = nc.scalar.copy
+        on_v = nc.vector.tensor_copy
+        on_g = nc.gpsimd.tensor_copy
         picked = [sb.tile([P, 2, S], U32, name="picked%d" % g) for g in range(PASSES)]
 
-        def gather(dst, g, u, a, b):
-            nc.vector.tensor_copy(dst, pairs[g, u][:].bitcast(U32).indirect(offs_sb[:, a // 16 : b // 16]))
+        def gather(i, a, b):
+            nc.vector.tensor_copy(picked[i // 2][:, i % 2, a:b], pairs[i][:].bitcast(U32).indirect(offs_sb[:, a // 16 : b // 16]))
 
-        codes = [sb.tile([P, S], U32, name="codes%d" % g, align_bytes=64) for g in range(PASSES)]
-        scales = [sb.tile([P, S], U8, name="scales%d" % g, align_bytes=64) for g in range(PASSES)]
-
-        def weave(g, a, b, tag):
-            woven = sb.tile([P, 4 * (b - a)], BF16, name="woven%d_%d" % (g, a), tag=tag, align_bytes=64)
-            nc.scalar.copy(woven[:].bitcast(U32).rearrange("p (s u) -> p s u", u=2), picked[g][:, :, a:b].rearrange("p u s -> p s u"))
-            return woven
-
-        def quantize(g, woven, a, b):
-            nc.vector.quantize_mx(out=codes[g][:, a:b].bitcast(FP8X4), scales=scales[g][:, a:b], in_=woven[:])
-
+        codes = {}
+        scales = {}
         woven = {}
-        cast(0)
-        gather(picked[0][:, 0, :], 0, 0, 0, S)
-        cast(1)
-        cast(2)
-        for a, b in FIRST_SLICES:
-            gather(picked[0][:, 1, a:b], 0, 1, a, b)
-        for i, (a, b) in enumerate(FIRST_SLICES):
-            woven[0, a] = weave(0, a, b, "first%d" % a)
-            cast(3 + i)
-            quantize(0, woven[0, a], a, b)
-        gather(picked[1][:, 0, :], 1, 0, 0, S)
-        cast(5)
-        cast(6)
+
+        def room(g, a, b, tag=None):
+            woven[g, a, b] = sb.tile([P, 4 * (b - a)], BF16, name="woven%d_%d" % (g, a), tag=tag or "woven%d_%d" % (g, a), align_bytes=64)
+
+        def weave(copy, g, a, b, word=U32):
+            copy(part(woven, g, a, b, 4).bitcast(word).rearrange("p (s u) -> p s u", u=2), picked[g][:, :, a:b].bitcast(word).rearrange("p u s -> p s u"))
+
+        def planes(g, a, b, tag=None):
+            codes[g, a, b] = sb.tile([P, b - a], U32, name="codes%d_%d" % (g, a), tag=tag or "codes%d_%d" % (g, a), align_bytes=64)
+            scales[g, a, b] = sb.tile([P, b - a], U8, name="scales%d_%d" % (g, a), align_bytes=64)
+
+        def part(tiles, g, a, b, width=1):
+            first, tile = [(lo, tile) for (h, lo, hi), tile in tiles.items() if h == g and lo <= a and b <= hi][0]
+            return tile[:, width * (a - first) : width * (b - first)]
+
+        def quantize(g, a, b):
+            nc.vector.quantize_mx(out=part(codes, g, a, b).bitcast(FP8X4), scales=part(scales, g, a, b), in_=part(woven, g, a, b, 4))
 
         banks = {}
         for a, b in LAST_SLICES:
             banks[0, a] = psum.tile([P, b - a], F32, name="bank0_%d" % a)
-        banks[1, 0] = psum.tile([P, S], F32, name="bank1")
+        for a, b in ROW1_SLICES:
+            banks[1, a] = psum.tile([P, b - a], F32, name="bank1_%d" % a)
 
         def product(m, g, a, b):
-            cols = slice(m * P, (m + 1) * P)
+            rows = slice(m * P, (m + 1) * P)
             nc.tensor.matmul_mx(
                 out=banks[m, a][:],
-                lhsT=w_words[:, g, cols].bitcast(FP8X4),
-                lhsT_scale=w_scales[:, g, cols],
-                rhs=codes[g][:, a:b].bitcast(FP8X4),
-                rhs_scale=scales[g][:, a:b],
+                lhsT=w_words[:, g, rows].bitcast(FP8X4),
+                lhsT_scale=w_scales[:, g, rows],
+                rhs=part(codes, g, a, b).bitcast(FP8X4),
+                rhs_scale=part(scales, g, a, b),
                 start=(g == 0),
                 stop=(g == PASSES - 1),
             )
 
         y = [sb.tile([P, S], F32, name="y%d" % m) for m in range(2)]
+
+        def drain(copy, m, a, b):
+            copy(y[m][:, a:b], banks[m, a][:])
+
+        cast(on_s, 0, 0, 400)
+        cast(on_v, 0, 400, 512)
+        cast(on_v, 0, 512, 1024)
+        gather(0, 0, S)
+        cast(on_s, 1, 0, 512)
+        cast(on_v, 1, 512, 864)
+        cast(on_s, 1, 864, 1024)
+        gather(1, 0, 256)
+        gather(1, 256, 512)
+        room(0, 0, 256)
+        room(0, 256, 512)
+        weave(on_v, 0, 0, 256, I32)
+        weave(on_v, 0, 256, 512, I32)
+        planes(0, 0, 512)
+        quantize(0, 0, 256)
+        quantize(0, 256, 512)
+        cast(on_s, 2, 0, 256)
+        cast(on_s, 2, 256, 640)
+        cast(on_s, 2, 640, 1024)
+        gather(2, 0, S)
+        cast(on_s, 3, 0, 384)
+        cast(on_s, 3, 384, 768)
+        cast(on_v, 3, 768, 1024)
+        planes(1, 0, 512)
         for a, b in LAST_SLICES:
             product(0, 0, a, b)
-        product(1, 0, 0, S)
+        for a, b in ROW1_SLICES:
+            product(1, 0, a, b)
         for a, b in LAST_SLICES:
-            gather(picked[1][:, 1, a:b], 1, 1, a, b)
-            woven[1, a] = weave(1, a, b, "woven%d" % a)
+            gather(3, a, b)
+            room(1, a, b)
+            weave(on_s, 1, a, b)
         for a, b in LAST_SLICES:
-            quantize(1, woven[1, a], a, b)
+            quantize(1, a, b)
             product(0, 1, a, b)
-            nc.scalar.copy(y[0][:, a:b], banks[0, a][:])
-        product(1, 1, 0, S)
-        nc.scalar.copy(y[1][:], banks[1, 0][:])
+            drain(on_s, 0, a, b)
+        for a, b in ROW1_SLICES:
+            product(1, 1, a, b)
+            drain(on_s, 1, a, b)
 
-        f_left = sb.tile([P, V], F32, name="f_left", tag="woven384", align_bytes=64)
+        f_left = sb.tile([P, V], F32, name="f_left", tag="woven1_384", align_bytes=64)
         nc.vector.tensor_scalar(f_left[:], f_right[:], -1.0, 1.0, MULT, ADD)
         lo = [sb.tile([P, V], F32, name="lo%d" % m) for m in range(2)]
         hi = [sb.tile([P, V], F32, name="hi%d" % m) for m in range(2)]
@@ -147,6 +184,6 @@ def tile_picked_lerp_none_e_kernel(tc, xT, w1_words, w1_scales, frac, offs, left
             nc.vector.tensor_tensor(hi[m][:], y[m][:].indirect(right_sb[:]), f_right[:], MULT)
             nc.vector.tensor_tensor(lo[m][:], y[m][:].indirect(left_sb[:]), f_left[:], MULT)
         for m in range(2):
-            res = sb.tile([P, V], F32, name="res%d" % m, tag=("woven384", "res1")[m], align_bytes=64)
+            res = sb.tile([P, V], F32, name="res%d" % m, tag=("woven1_384", "res1")[m], align_bytes=64)
             nc.vector.tensor_tensor(res[:], lo[m][:], hi[m][:], ADD)
             nc.sync.dma_start(out[m * P : (m + 1) * P, :], res[:])

@@ -18,16 +18,14 @@ ADD = mybir.AluOpType.add
 P = 128
 PASSES = 2
 LOADS = (
-    (0, "run", 0, 1536),
-    (0, "run", 1536, 2048),
-    (1, "cols", 0, 512),
-    (1, "cols", 512, 1024),
-    (2, "cols", 0, 256),
-    (2, "cols", 256, 640),
-    (2, "cols", 640, 1024),
-    (3, "cols", 0, 384),
-    (3, "cols", 384, 768),
-    (3, "cols", 768, 1024),
+    (0, "run", 0, 2048),
+    (1, "run", 0, 1408),
+    (1, "run", 1408, 2048),
+    (2, "run", 0, 1408),
+    (2, "run", 1408, 2048),
+    (3, "run", 0, 1280),
+    (3, "run", 1280, 1664),
+    (3, "run", 1664, 2048),
 )
 LAST_SLICES = ((0, 128), (128, 256), (256, 384), (384, 512),)
 ROW1_SLICES = ((0, 512),)
@@ -136,13 +134,12 @@ def tile_picked_lerp_none_e_kernel(tc, xT, w1_words, w1_scales, frac, offs, left
         def drain(copy, m, a, b):
             copy(y[m][:, a:b], banks[m, a][:])
 
-        cast(on_s, 0, 0, 400)
-        cast(on_v, 0, 400, 512)
-        cast(on_v, 0, 512, 1024)
+        cast(on_s, 0, 0, 384)
+        cast(on_v, 0, 384, 1024)
         gather(0, 0, S)
-        cast(on_s, 1, 0, 512)
-        cast(on_v, 1, 512, 864)
-        cast(on_s, 1, 864, 1024)
+        cast(on_s, 1, 0, 384)
+        cast(on_v, 1, 384, 800)
+        cast(on_s, 1, 800, 1024)
         gather(1, 0, 256)
         gather(1, 256, 512)
         room(0, 0, 256)
@@ -152,13 +149,14 @@ def tile_picked_lerp_none_e_kernel(tc, xT, w1_words, w1_scales, frac, offs, left
         planes(0, 0, 512)
         quantize(0, 0, 256)
         quantize(0, 256, 512)
-        cast(on_s, 2, 0, 256)
-        cast(on_s, 2, 256, 640)
-        cast(on_s, 2, 640, 1024)
+        cast(on_s, 2, 0, 384)
+        cast(on_s, 2, 384, 896)
+        cast(on_v, 2, 896, 1024)
         gather(2, 0, S)
-        cast(on_s, 3, 0, 384)
-        cast(on_s, 3, 384, 768)
-        cast(on_v, 3, 768, 1024)
+        cast(on_s, 3, 0, 256)
+        cast(on_s, 3, 256, 640)
+        cast(on_s, 3, 640, 800)
+        cast(on_v, 3, 800, 1024)
         planes(1, 0, 512)
         for a, b in LAST_SLICES:
             product(0, 0, a, b)

@@ -27,8 +27,10 @@ LOADS = (
     (3, "run", 1280, 1664),
     (3, "run", 1664, 2048),
 )
+PAD = 496
 LAST_SLICES = ((0, 128), (128, 256), (256, 384), (384, 512),)
-ROW1_SLICES = ((0, 512),)
+ROW0_SLICES = ((0, 128), (128, 256), (256, 384), (384, 512),)
+ROW1_SLICES = ((0, 256), (256, 512),)
 
 
 def tile_picked_lerp_none_e_kernel(tc, xT, w1_words, w1_scales, frac, offs, left, right, out):
@@ -44,22 +46,24 @@ def tile_picked_lerp_none_e_kernel(tc, xT, w1_words, w1_scales, frac, offs, left
 
         x_runs = xT.rearrange("(g p u e) t -> g u p (e t)", g=PASSES, u=2, e=2)
         x_rows = xT.rearrange("(g p u e) t -> g u p e t", g=PASSES, u=2, e=2)
-        pairs = [sb.tile([P, 2 * T], BF16, name="pairs%d" % i, align_bytes=64) for i in range(4)]
+        pairs = [sb.tile([P, 2 * T], BF16, name="pairs%d" % i, tag="pairs%d" % i, align_bytes=64) for i in range(4)]
         w_words = sb.tile([P, PASSES, N], U32, name="w_words", align_bytes=64)
         w_scales = sb.tile([P, PASSES, N], U8, name="w_scales", align_bytes=64)
         f_right = sb.tile([P, V], F32, name="f_right")
 
         runs = {}
         cols = []
+        padded = {}
         for c, (i, kind, a, b) in enumerate(LOADS):
             if kind == "run":
                 if i not in runs:
-                    runs[i] = sb.tile([P, 2 * T], F32, name="run%d" % i, align_bytes=64)
+                    runs[i] = sb.tile([P, 2 * T + (240 if i == 3 else 0)], F32, name="run%d" % i, tag="run%d" % i, align_bytes=64)
                 nc.sync.dma_start(runs[i][:, a:b], x_runs[i // 2, i % 2][:, a:b])
             else:
-                piece = sb.tile([P, 2, b - a], F32, name="cols%d" % c, tag="cols%d" % c, align_bytes=64)
+                padded[c] = sb.tile([P, 2 * PAD + 2 * (b - a)], F32, name="cols%d" % c, tag="cols%d" % c, align_bytes=64)
+                piece = padded[c][:, PAD : PAD + 2 * (b - a)].rearrange("p (e t) -> p e t", e=2)
                 cols.append((i, a, b, piece))
-                nc.sync.dma_start(piece[:], x_rows[i // 2, i % 2][:, :, a:b])
+                nc.sync.dma_start(piece, x_rows[i // 2, i % 2][:, :, a:b])
             if c == 0:
                 nc.sync.dma_start(offs_sb[:], offs)
 
@@ -77,18 +81,23 @@ def tile_picked_lerp_none_e_kernel(tc, xT, w1_words, w1_scales, frac, offs, left
         def cast(copy, i, a, b):
             dst = pairs[i][:].rearrange("p (t e) -> p t e", e=2)[:, a:b, :]
             if i in runs:
-                copy(dst, runs[i][:].rearrange("p (e t) -> p t e", e=2)[:, a:b, :])
+                copy(dst, runs[i][:, 0 : 2 * T].rearrange("p (e t) -> p t e", e=2)[:, a:b, :])
             else:
                 first, piece = [(lo, piece) for j, lo, hi, piece in cols if j == i and lo <= a and b <= hi][0]
-                copy(dst, piece[:].rearrange("p e t -> p t e")[:, a - first : b - first, :])
+                copy(dst, piece.rearrange("p e t -> p t e")[:, a - first : b - first, :])
 
         on_s = nc.scalar.copy
         on_v = nc.vector.tensor_copy
         on_g = nc.gpsimd.tensor_copy
-        picked = [sb.tile([P, 2, S], U32, name="picked%d" % g) for g in range(PASSES)]
+        picked = [sb.tile([P, 2, S], U32, name="picked%d" % g, tag="picked%d" % g, align_bytes=64) for g in range(PASSES)]
+
+        late = runs[3][:, 2 * T - 16 :].bitcast(U32).rearrange("p (u s) -> p u s", u=2)
+
+        def words(g, a, b):
+            return late if (g, a) == (1, 384) else picked[g][:, :, a:b]
 
         def gather(i, a, b):
-            nc.vector.tensor_copy(picked[i // 2][:, i % 2, a:b], pairs[i][:].bitcast(U32).indirect(offs_sb[:, a // 16 : b // 16]))
+            nc.vector.tensor_copy(words(i // 2, a, b)[:, i % 2, :], pairs[i][:].bitcast(U32).indirect(offs_sb[:, a // 16 : b // 16]))
 
         codes = {}
         scales = {}
@@ -97,11 +106,30 @@ def tile_picked_lerp_none_e_kernel(tc, xT, w1_words, w1_scales, frac, offs, left
         def room(g, a, b, tag=None):
             woven[g, a, b] = sb.tile([P, 4 * (b - a)], BF16, name="woven%d_%d" % (g, a), tag=tag or "woven%d_%d" % (g, a), align_bytes=64)
 
+        def room_in(g, a, b, i, first):
+            woven[g, a, b] = runs[i][:, first : first + 2 * (b - a)].bitcast(BF16)
+
+        def room_front(g, a, b, c):
+            woven[g, a, b] = padded[c][:, 0 : 2 * (b - a)].bitcast(BF16)
+
+        def room_back(g, a, b, c):
+            end = padded[c].shape[1]
+            woven[g, a, b] = padded[c][:, end - 2 * (b - a) : end].bitcast(BF16)
+
         def weave(copy, g, a, b, word=U32):
-            copy(part(woven, g, a, b, 4).bitcast(word).rearrange("p (s u) -> p s u", u=2), picked[g][:, :, a:b].bitcast(word).rearrange("p u s -> p s u"))
+            copy(part(woven, g, a, b, 4).bitcast(word).rearrange("p (s u) -> p s u", u=2), words(g, a, b).bitcast(word).rearrange("p u s -> p s u"))
+
+        def weave_values(g, a, b):
+            dst = part(woven, g, a, b, 4).rearrange("p (s u e) -> p s u e", u=2, e=2)
+            src = picked[g][:].rearrange("p u s -> p (u s)").bitcast(BF16).rearrange("p (u s e) -> p s u e", u=2, e=2)
+            nc.vector.tensor_copy(dst, src[:, a:b, :, :])
 
         def planes(g, a, b, tag=None):
             codes[g, a, b] = sb.tile([P, b - a], U32, name="codes%d_%d" % (g, a), tag=tag or "codes%d_%d" % (g, a), align_bytes=64)
+            scales[g, a, b] = sb.tile([P, b - a], U8, name="scales%d_%d" % (g, a), align_bytes=64)
+
+        def planes_in(g, a, b, i, first):
+            codes[g, a, b] = runs[i][:, first : first + b - a].bitcast(U32)
             scales[g, a, b] = sb.tile([P, b - a], U8, name="scales%d_%d" % (g, a), align_bytes=64)
 
         def part(tiles, g, a, b, width=1):
@@ -112,21 +140,20 @@ def tile_picked_lerp_none_e_kernel(tc, xT, w1_words, w1_scales, frac, offs, left
             nc.vector.quantize_mx(out=part(codes, g, a, b).bitcast(FP8X4), scales=part(scales, g, a, b), in_=part(woven, g, a, b, 4))
 
         banks = {}
-        for a, b in LAST_SLICES:
-            banks[0, a] = psum.tile([P, b - a], F32, name="bank0_%d" % a)
-        for a, b in ROW1_SLICES:
-            banks[1, a] = psum.tile([P, b - a], F32, name="bank1_%d" % a)
 
-        def product(m, g, a, b):
+        def bank(m, a, b, tag=None):
+            banks[m, a] = psum.tile([P, b - a], F32, name="bank%d_%d" % (m, a), tag=tag or "bank%d_%d" % (m, a))
+
+        def product(m, g, a, b, first=None, last=None, base=None):
             rows = slice(m * P, (m + 1) * P)
             nc.tensor.matmul_mx(
-                out=banks[m, a][:],
+                out=banks[m, a][:] if base is None else banks[m, base][:, a - base : b - base],
                 lhsT=w_words[:, g, rows].bitcast(FP8X4),
                 lhsT_scale=w_scales[:, g, rows],
                 rhs=part(codes, g, a, b).bitcast(FP8X4),
                 rhs_scale=part(scales, g, a, b),
-                start=(g == 0),
-                stop=(g == PASSES - 1),
+                start=(g == 0) if first is None else first,
+                stop=(g == PASSES - 1) if last is None else last,
             )
 
         y = [sb.tile([P, S], F32, name="y%d" % m) for m in range(2)]
@@ -144,23 +171,27 @@ def tile_picked_lerp_none_e_kernel(tc, xT, w1_words, w1_scales, frac, offs, left
         gather(1, 256, 512)
         room(0, 0, 256)
         room(0, 256, 512)
-        weave(on_v, 0, 0, 256, I32)
-        weave(on_v, 0, 256, 512, I32)
+        weave_values(0, 0, 256)
+        weave_values(0, 256, 512)
         planes(0, 0, 512)
         quantize(0, 0, 256)
         quantize(0, 256, 512)
         cast(on_s, 2, 0, 384)
-        cast(on_s, 2, 384, 896)
-        cast(on_v, 2, 896, 1024)
-        gather(2, 0, S)
+        cast(on_s, 2, 384, 864)
+        cast(on_v, 2, 864, 1024)
+        gather(2, 0, 384)
         cast(on_s, 3, 0, 256)
         cast(on_s, 3, 256, 640)
-        cast(on_s, 3, 640, 800)
-        cast(on_v, 3, 800, 1024)
+        cast(on_s, 3, 640, 720)
+        cast(on_v, 3, 992, 1024)
+        cast(on_v, 3, 720, 992)
+        gather(2, 384, S)
         planes(1, 0, 512)
         for a, b in LAST_SLICES:
+            bank(0, a, b)
             product(0, 0, a, b)
         for a, b in ROW1_SLICES:
+            bank(1, a, b)
             product(1, 0, a, b)
         for a, b in LAST_SLICES:
             gather(3, a, b)

@@ -23,11 +23,12 @@ LOADS = (
     (1, "run", 1408, 2048),
     (2, "run", 0, 1408),
     (2, "run", 1408, 2048),
-    (3, "run", 0, 1280),
-    (3, "run", 1280, 1664),
-    (3, "run", 1664, 2048),
+    (3, "run", 0, 1472),
+    (3, "run", 1472, 1920),
+    (3, "run", 1920, 2048),
 )
 PAD = 496
+LATE = 208
 LAST_SLICES = ((0, 128), (128, 256), (256, 384), (384, 512),)
 ROW0_SLICES = ((0, 128), (128, 256), (256, 384), (384, 512),)
 ROW1_SLICES = ((0, 256), (256, 512),)
@@ -57,7 +58,7 @@ def tile_picked_lerp_none_e_kernel(tc, xT, w1_words, w1_scales, frac, offs, left
         for c, (i, kind, a, b) in enumerate(LOADS):
             if kind == "run":
                 if i not in runs:
-                    runs[i] = sb.tile([P, 2 * T + (240 if i == 3 else 0)], F32, name="run%d" % i, tag="run%d" % i, align_bytes=64)
+                    runs[i] = sb.tile([P, 2 * T], F32, name="run%d" % i, tag="run%d" % i, align_bytes=64)
                 nc.sync.dma_start(runs[i][:, a:b], x_runs[i // 2, i % 2][:, a:b])
             else:
                 padded[c] = sb.tile([P, 2 * PAD + 2 * (b - a)], F32, name="cols%d" % c, tag="cols%d" % c, align_bytes=64)
@@ -88,10 +89,13 @@ def tile_picked_lerp_none_e_kernel(tc, xT, w1_words, w1_scales, frac, offs, left
 
         on_s = nc.scalar.copy
         on_v = nc.vector.tensor_copy
-        on_g = nc.gpsimd.tensor_copy
+
+        def on_g(dst, src):
+            nc.gpsimd.tensor_scalar(dst, src, 1.0, 0.0, MULT, ADD)
+
         picked = [sb.tile([P, 2, S], U32, name="picked%d" % g, tag="picked%d" % g, align_bytes=64) for g in range(PASSES)]
 
-        late = runs[3][:, 2 * T - 16 :].bitcast(U32).rearrange("p (u s) -> p u s", u=2)
+        late = runs[3][:, LATE : LATE + 256].bitcast(U32).rearrange("p (u s) -> p u s", u=2)
 
         def words(g, a, b):
             return late if (g, a) == (1, 384) else picked[g][:, :, a:b]
@@ -180,11 +184,11 @@ def tile_picked_lerp_none_e_kernel(tc, xT, w1_words, w1_scales, frac, offs, left
         cast(on_s, 2, 384, 864)
         cast(on_v, 2, 864, 1024)
         gather(2, 0, 384)
-        cast(on_s, 3, 0, 256)
-        cast(on_s, 3, 256, 640)
-        cast(on_s, 3, 640, 720)
-        cast(on_v, 3, 992, 1024)
-        cast(on_v, 3, 720, 992)
+        cast(on_g, 3, 0, 160)
+        cast(on_s, 3, 160, 448)
+        cast(on_s, 3, 448, 608)
+        cast(on_v, 3, 608, 896)
+        cast(on_s, 3, 896, 1024)
         gather(2, 384, S)
         planes(1, 0, 512)
         for a, b in LAST_SLICES:

@@ -28,6 +28,7 @@ LOADS = (
     (3, "run", 1920, 2048),
 )
 PAD = 496
+FRONT = (0, 0, 1008, 0)
 LATE = 208
 LAST_SLICES = ((0, 128), (128, 256), (256, 384), (384, 512),)
 ROW0_SLICES = ((0, 128), (128, 256), (256, 384), (384, 512),)
@@ -58,8 +59,8 @@ def tile_picked_lerp_none_e_kernel(tc, xT, w1_words, w1_scales, frac, offs, left
         for c, (i, kind, a, b) in enumerate(LOADS):
             if kind == "run":
                 if i not in runs:
-                    runs[i] = sb.tile([P, 2 * T], F32, name="run%d" % i, tag="run%d" % i, align_bytes=64)
-                nc.sync.dma_start(runs[i][:, a:b], x_runs[i // 2, i % 2][:, a:b])
+                    runs[i] = sb.tile([P, FRONT[i] + 2 * T], F32, name="run%d" % i, tag="run%d" % i, align_bytes=64)
+                nc.sync.dma_start(runs[i][:, FRONT[i] + a : FRONT[i] + b], x_runs[i // 2, i % 2][:, a:b])
             else:
                 padded[c] = sb.tile([P, 2 * PAD + 2 * (b - a)], F32, name="cols%d" % c, tag="cols%d" % c, align_bytes=64)
                 piece = padded[c][:, PAD : PAD + 2 * (b - a)].rearrange("p (e t) -> p e t", e=2)
@@ -82,7 +83,7 @@ def tile_picked_lerp_none_e_kernel(tc, xT, w1_words, w1_scales, frac, offs, left
         def cast(copy, i, a, b):
             dst = pairs[i][:].rearrange("p (t e) -> p t e", e=2)[:, a:b, :]
             if i in runs:
-                copy(dst, runs[i][:, 0 : 2 * T].rearrange("p (e t) -> p t e", e=2)[:, a:b, :])
+                copy(dst, runs[i][:, FRONT[i] : FRONT[i] + 2 * T].rearrange("p (e t) -> p t e", e=2)[:, a:b, :])
             else:
                 first, piece = [(lo, piece) for j, lo, hi, piece in cols if j == i and lo <= a and b <= hi][0]
                 copy(dst, piece.rearrange("p e t -> p t e")[:, a - first : b - first, :])
@@ -173,21 +174,20 @@ def tile_picked_lerp_none_e_kernel(tc, xT, w1_words, w1_scales, frac, offs, left
         cast(on_s, 1, 800, 1024)
         gather(1, 0, 256)
         gather(1, 256, 512)
-        room(0, 0, 256)
-        room(0, 256, 512)
-        weave_values(0, 0, 256)
-        weave_values(0, 256, 512)
+        room_in(0, 0, 512, 2, 0)
+        weave(on_v, 0, 0, 256, I32)
+        cast(on_s, 2, 0, 256)
+        weave(on_v, 0, 256, 512, I32)
+        cast(on_s, 2, 256, 384)
+        cast(on_v, 2, 800, 1024)
+        cast(on_s, 2, 384, 800)
         planes(0, 0, 512)
-        quantize(0, 0, 256)
-        quantize(0, 256, 512)
-        cast(on_s, 2, 0, 384)
-        cast(on_s, 2, 384, 864)
-        cast(on_v, 2, 864, 1024)
+        quantize(0, 0, 512)
         gather(2, 0, 384)
-        cast(on_g, 3, 0, 160)
-        cast(on_s, 3, 160, 448)
-        cast(on_s, 3, 448, 608)
-        cast(on_v, 3, 608, 896)
+        cast(on_g, 3, 0, 176)
+        cast(on_s, 3, 176, 448)
+        cast(on_s, 3, 448, 560)
+        cast(on_v, 3, 560, 896)
         cast(on_s, 3, 896, 1024)
         gather(2, 384, S)
         planes(1, 0, 512)

@@ -18,9 +18,10 @@ ADD = mybir.AluOpType.add
 P = 128
 PASSES = 2
 LOADS = (
-    (0, "run", 0, 2048),
-    (1, "run", 0, 1408),
-    (1, "run", 1408, 2048),
+    (0, "run", 0, 1536),
+    (0, "run", 1536, 2048),
+    (1, "run", 0, 1536),
+    (1, "run", 1536, 2048),
     (2, "run", 0, 1408),
     (2, "run", 1408, 2048),
     (3, "run", 0, 1472),
@@ -48,7 +49,7 @@ def tile_picked_lerp_none_e_kernel(tc, xT, w1_words, w1_scales, frac, offs, left
 
         x_runs = xT.rearrange("(g p u e) t -> g u p (e t)", g=PASSES, u=2, e=2)
         x_rows = xT.rearrange("(g p u e) t -> g u p e t", g=PASSES, u=2, e=2)
-        pairs = [sb.tile([P, 2 * T], BF16, name="pairs%d" % i, tag="pairs%d" % i, align_bytes=64) for i in range(4)]
+        pairs = {i: sb.tile([P, 2 * T], BF16, name="pairs%d" % i, tag="pairs%d" % i, align_bytes=64) for i in (0, 2, 3)}
         w_words = sb.tile([P, PASSES, N], U32, name="w_words", align_bytes=64)
         w_scales = sb.tile([P, PASSES, N], U8, name="w_scales", align_bytes=64)
         f_right = sb.tile([P, V], F32, name="f_right")
@@ -166,26 +167,30 @@ def tile_picked_lerp_none_e_kernel(tc, xT, w1_words, w1_scales, frac, offs, left
         def drain(copy, m, a, b):
             copy(y[m][:, a:b], banks[m, a][:])
 
-        cast(on_s, 0, 0, 384)
-        cast(on_v, 0, 384, 1024)
+        cast(on_s, 0, 0, 176)
+        cast(on_v, 0, 176, 512)
+        cast(on_v, 0, 512, 848)
+        cast(on_s, 0, 848, 1024)
         gather(0, 0, S)
-        cast(on_s, 1, 0, 384)
-        cast(on_v, 1, 384, 800)
-        cast(on_s, 1, 800, 1024)
+        pairs[1] = sb.tile([P, 2 * T], BF16, name="pairs1", tag="run0", align_bytes=64)
+        cast(on_s, 1, 0, 240)
+        cast(on_v, 1, 240, 512)
+        cast(on_v, 1, 512, 848)
+        cast(on_s, 1, 848, 1024)
         gather(1, 0, 256)
         gather(1, 256, 512)
         room_in(0, 0, 512, 2, 0)
         weave(on_v, 0, 0, 256, I32)
-        cast(on_s, 2, 0, 256)
+        cast(on_s, 2, 0, 208)
         weave(on_v, 0, 256, 512, I32)
-        cast(on_s, 2, 256, 384)
-        cast(on_v, 2, 800, 1024)
-        cast(on_s, 2, 384, 800)
+        cast(on_s, 2, 208, 384)
+        cast(on_v, 2, 768, 1024)
+        cast(on_s, 2, 384, 768)
         planes(0, 0, 512)
         quantize(0, 0, 512)
         gather(2, 0, 384)
-        cast(on_g, 3, 0, 176)
-        cast(on_s, 3, 176, 448)
+        cast(on_g, 3, 0, 192)
+        cast(on_s, 3, 192, 448)
         cast(on_s, 3, 448, 560)
         cast(on_v, 3, 560, 896)
         cast(on_s, 3, 896, 1024)

@@ -17,23 +17,10 @@ ADD = mybir.AluOpType.add
 
 P = 128
 PASSES = 2
-LOADS = (
-    (0, "run", 0, 1536),
-    (0, "run", 1536, 2048),
-    (1, "run", 0, 1536),
-    (1, "run", 1536, 2048),
-    (2, "run", 0, 1408),
-    (2, "run", 1408, 2048),
-    (3, "run", 0, 1472),
-    (3, "run", 1472, 1920),
-    (3, "run", 1920, 2048),
-)
-PAD = 496
-FRONT = (0, 0, 1008, 0)
-LATE = 208
-LAST_SLICES = ((0, 128), (128, 256), (256, 384), (384, 512),)
-ROW0_SLICES = ((0, 128), (128, 256), (256, 384), (384, 512),)
-ROW1_SLICES = ((0, 256), (256, 512),)
+SLICE = 128
+CUTS = {1: (512,), 2: (384,), 3: (384, 896)}
+FRONT = {1: 0, 2: 496, 3: 0}
+LATE = 144
 
 
 def tile_picked_lerp_none_e_kernel(tc, xT, w1_words, w1_scales, frac, offs, left, right, out):
@@ -48,28 +35,20 @@ def tile_picked_lerp_none_e_kernel(tc, xT, w1_words, w1_scales, frac, offs, left
         right_sb = lists.tile([P, V // 16], U16, name="right_sb")
 
         x_runs = xT.rearrange("(g p u e) t -> g u p (e t)", g=PASSES, u=2, e=2)
-        x_rows = xT.rearrange("(g p u e) t -> g u p e t", g=PASSES, u=2, e=2)
-        pairs = {i: sb.tile([P, 2 * T], BF16, name="pairs%d" % i, tag="pairs%d" % i, align_bytes=64) for i in (0, 2, 3)}
+        rows = [sb.tile([P, T], F32, name="row%d" % e, tag="row%d" % e, align_bytes=64) for e in range(2)]
+        nc.sync.dma_start(rows[0][:], x_runs[0, 0][:, 0:T])
+        nc.sync.dma_start(offs_sb[:], offs)
+        nc.sync.dma_start(rows[1][:], x_runs[0, 0][:, T : 2 * T])
+        runs = {}
+        for i in (1, 2, 3):
+            runs[i] = sb.tile([P, FRONT[i] + 2 * T], F32, name="run%d" % i, align_bytes=64)
+            ends = [0] + [T + frames for frames in CUTS[i]] + [2 * T]
+            for a, b in zip(ends, ends[1:]):
+                nc.sync.dma_start(runs[i][:, FRONT[i] + a : FRONT[i] + b], x_runs[i // 2, i % 2][:, a:b])
+
         w_words = sb.tile([P, PASSES, N], U32, name="w_words", align_bytes=64)
         w_scales = sb.tile([P, PASSES, N], U8, name="w_scales", align_bytes=64)
-        f_right = sb.tile([P, V], F32, name="f_right")
-
-        runs = {}
-        cols = []
-        padded = {}
-        for c, (i, kind, a, b) in enumerate(LOADS):
-            if kind == "run":
-                if i not in runs:
-                    runs[i] = sb.tile([P, FRONT[i] + 2 * T], F32, name="run%d" % i, tag="run%d" % i, align_bytes=64)
-                nc.sync.dma_start(runs[i][:, FRONT[i] + a : FRONT[i] + b], x_runs[i // 2, i % 2][:, a:b])
-            else:
-                padded[c] = sb.tile([P, 2 * PAD + 2 * (b - a)], F32, name="cols%d" % c, tag="cols%d" % c, align_bytes=64)
-                piece = padded[c][:, PAD : PAD + 2 * (b - a)].rearrange("p (e t) -> p e t", e=2)
-                cols.append((i, a, b, piece))
-                nc.sync.dma_start(piece, x_rows[i // 2, i % 2][:, :, a:b])
-            if c == 0:
-                nc.sync.dma_start(offs_sb[:], offs)
-
+        f_right = sb.tile([P, V], F32, name="f_right", tag="f_right")
         nc.gpsimd.memset(w_scales[:].rearrange("p g n -> p (g n)").bitcast(I32), 0)
         for q in range(4):
             nc.sync.dma_start(
@@ -81,138 +60,109 @@ def tile_picked_lerp_none_e_kernel(tc, xT, w1_words, w1_scales, frac, offs, left
         nc.sync.dma_start(right_sb[:], right)
         nc.sync.dma_start(left_sb[:], left)
 
-        def cast(copy, i, a, b):
-            dst = pairs[i][:].rearrange("p (t e) -> p t e", e=2)[:, a:b, :]
-            if i in runs:
-                copy(dst, runs[i][:, FRONT[i] : FRONT[i] + 2 * T].rearrange("p (e t) -> p t e", e=2)[:, a:b, :])
-            else:
-                first, piece = [(lo, piece) for j, lo, hi, piece in cols if j == i and lo <= a and b <= hi][0]
-                copy(dst, piece.rearrange("p e t -> p t e")[:, a - first : b - first, :])
-
         on_s = nc.scalar.copy
         on_v = nc.vector.tensor_copy
 
         def on_g(dst, src):
             nc.gpsimd.tensor_scalar(dst, src, 1.0, 0.0, MULT, ADD)
 
-        picked = [sb.tile([P, 2, S], U32, name="picked%d" % g, tag="picked%d" % g, align_bytes=64) for g in range(PASSES)]
+        def entries(a, b):
+            return offs_sb[:, a // 16 : b // 16]
 
-        late = runs[3][:, LATE : LATE + 256].bitcast(U32).rearrange("p (u s) -> p u s", u=2)
+        pairs = {}
 
-        def words(g, a, b):
-            return late if (g, a) == (1, 384) else picked[g][:, :, a:b]
+        def cast(copy, i, a, b):
+            copy(pairs[i][:].rearrange("p (t e) -> p t e", e=2)[:, a:b, :], runs[i][:, FRONT[i] :].rearrange("p (e t) -> p t e", e=2)[:, a:b, :])
+
+        kept = sb.tile([P, 2, S], F32, name="kept", align_bytes=64)
+        woven0 = sb.tile([P, 2 * S], BF16, name="woven0", align_bytes=64)
+        woven0_late = runs[2][:, 0:512]
+        halves = sb.tile([P, 2, 256], U32, name="halves", align_bytes=64)
+        codes = [sb.tile([P, S], U32, name="codes%d" % g, align_bytes=64) for g in range(PASSES)]
+        scales = [sb.tile([P, S], U8, name="scales%d" % g, align_bytes=64) for g in range(PASSES)]
+
+        def quantize(g, values, a, b):
+            nc.vector.quantize_mx(out=codes[g][:, a:b].bitcast(FP8X4), scales=scales[g][:, a:b], in_=values)
+
+        def keep(e, a, b):
+            on_v(kept[:, e, a:b], rows[e][:].indirect(entries(a, b)))
+
+        def place(a, b):
+            on_s(woven0[:].rearrange("p (s t) -> p s t", t=4)[:, a:b, 0:2], kept[:].rearrange("p e s -> p s e")[:, a:b, :])
+
+        def gather_into_place(a, b):
+            on_v(woven0[:].bitcast(U32).rearrange("p (s u) -> p u s", u=2)[:, 1, a:b], pairs[1][:].bitcast(U32).indirect(entries(a, b)))
+
+        picked = sb.tile([P, 2, S], U32, name="picked", align_bytes=64)
+        late = runs[3][:, LATE : LATE + 2 * SLICE].bitcast(U32).rearrange("p (u s) -> p u s", u=2)
+
+        def words(a, b):
+            return late if a == S - SLICE else picked[:, :, a:b]
 
         def gather(i, a, b):
-            nc.vector.tensor_copy(words(i // 2, a, b)[:, i % 2, :], pairs[i][:].bitcast(U32).indirect(offs_sb[:, a // 16 : b // 16]))
+            on_v(words(a, b)[:, i % 2, :], pairs[i][:].bitcast(U32).indirect(entries(a, b)))
 
-        codes = {}
-        scales = {}
-        woven = {}
+        for i in (2, 3):
+            pairs[i] = sb.tile([P, 2 * T], BF16, name="pairs%d" % i, align_bytes=64)
 
-        def room(g, a, b, tag=None):
-            woven[g, a, b] = sb.tile([P, 4 * (b - a)], BF16, name="woven%d_%d" % (g, a), tag=tag or "woven%d_%d" % (g, a), align_bytes=64)
-
-        def room_in(g, a, b, i, first):
-            woven[g, a, b] = runs[i][:, first : first + 2 * (b - a)].bitcast(BF16)
-
-        def room_front(g, a, b, c):
-            woven[g, a, b] = padded[c][:, 0 : 2 * (b - a)].bitcast(BF16)
-
-        def room_back(g, a, b, c):
-            end = padded[c].shape[1]
-            woven[g, a, b] = padded[c][:, end - 2 * (b - a) : end].bitcast(BF16)
-
-        def weave(copy, g, a, b, word=U32):
-            copy(part(woven, g, a, b, 4).bitcast(word).rearrange("p (s u) -> p s u", u=2), words(g, a, b).bitcast(word).rearrange("p u s -> p s u"))
-
-        def weave_values(g, a, b):
-            dst = part(woven, g, a, b, 4).rearrange("p (s u e) -> p s u e", u=2, e=2)
-            src = picked[g][:].rearrange("p u s -> p (u s)").bitcast(BF16).rearrange("p (u s e) -> p s u e", u=2, e=2)
-            nc.vector.tensor_copy(dst, src[:, a:b, :, :])
-
-        def planes(g, a, b, tag=None):
-            codes[g, a, b] = sb.tile([P, b - a], U32, name="codes%d_%d" % (g, a), tag=tag or "codes%d_%d" % (g, a), align_bytes=64)
-            scales[g, a, b] = sb.tile([P, b - a], U8, name="scales%d_%d" % (g, a), align_bytes=64)
-
-        def planes_in(g, a, b, i, first):
-            codes[g, a, b] = runs[i][:, first : first + b - a].bitcast(U32)
-            scales[g, a, b] = sb.tile([P, b - a], U8, name="scales%d_%d" % (g, a), align_bytes=64)
-
-        def part(tiles, g, a, b, width=1):
-            first, tile = [(lo, tile) for (h, lo, hi), tile in tiles.items() if h == g and lo <= a and b <= hi][0]
-            return tile[:, width * (a - first) : width * (b - first)]
-
-        def quantize(g, a, b):
-            nc.vector.quantize_mx(out=part(codes, g, a, b).bitcast(FP8X4), scales=part(scales, g, a, b), in_=part(woven, g, a, b, 4))
-
-        banks = {}
-
-        def bank(m, a, b, tag=None):
-            banks[m, a] = psum.tile([P, b - a], F32, name="bank%d_%d" % (m, a), tag=tag or "bank%d_%d" % (m, a))
-
-        def product(m, g, a, b, first=None, last=None, base=None):
-            rows = slice(m * P, (m + 1) * P)
-            nc.tensor.matmul_mx(
-                out=banks[m, a][:] if base is None else banks[m, base][:, a - base : b - base],
-                lhsT=w_words[:, g, rows].bitcast(FP8X4),
-                lhsT_scale=w_scales[:, g, rows],
-                rhs=part(codes, g, a, b).bitcast(FP8X4),
-                rhs_scale=part(scales, g, a, b),
-                start=(g == 0) if first is None else first,
-                stop=(g == PASSES - 1) if last is None else last,
-            )
-
-        y = [sb.tile([P, S], F32, name="y%d" % m) for m in range(2)]
-
-        def drain(copy, m, a, b):
-            copy(y[m][:, a:b], banks[m, a][:])
-
-        cast(on_s, 0, 0, 176)
-        cast(on_v, 0, 176, 512)
-        cast(on_v, 0, 512, 848)
-        cast(on_s, 0, 848, 1024)
-        gather(0, 0, S)
-        pairs[1] = sb.tile([P, 2 * T], BF16, name="pairs1", tag="run0", align_bytes=64)
-        cast(on_s, 1, 0, 240)
-        cast(on_v, 1, 240, 512)
-        cast(on_v, 1, 512, 848)
-        cast(on_s, 1, 848, 1024)
-        gather(1, 0, 256)
-        gather(1, 256, 512)
-        room_in(0, 0, 512, 2, 0)
-        weave(on_v, 0, 0, 256, I32)
-        cast(on_s, 2, 0, 208)
-        weave(on_v, 0, 256, 512, I32)
-        cast(on_s, 2, 208, 384)
+        keep(0, 0, S)
+        keep(1, 0, 256)
+        place(0, 256)
+        keep(1, 256, S)
+        on_s(halves[:, 0, :].bitcast(BF16).rearrange("p (s e) -> p s e", e=2), kept[:].rearrange("p e s -> p s e")[:, 256:S, :])
+        pairs[1] = sb.tile([P, 2 * T], BF16, name="pairs1", tag="row0", align_bytes=64)
+        cast(on_v, 1, 0, 512)
+        cast(on_v, 1, 512, 928)
+        cast(on_s, 1, 928, 1024)
+        gather_into_place(0, 256)
+        on_v(halves[:, 1, :], pairs[1][:].bitcast(U32).indirect(entries(256, S)))
+        quantize(0, woven0[:], 0, 256)
+        cast(on_s, 2, 0, 144)
+        on_v(woven0_late.bitcast(I32).rearrange("p (s u) -> p s u", u=2), halves[:].bitcast(I32).rearrange("p u s -> p s u"))
+        cast(on_g, 2, 304, 384)
+        cast(on_s, 2, 144, 304)
         cast(on_v, 2, 768, 1024)
         cast(on_s, 2, 384, 768)
-        planes(0, 0, 512)
-        quantize(0, 0, 512)
+        quantize(0, woven0_late.bitcast(BF16), 256, S)
         gather(2, 0, 384)
-        cast(on_g, 3, 0, 192)
-        cast(on_s, 3, 192, 448)
-        cast(on_s, 3, 448, 560)
-        cast(on_v, 3, 560, 896)
+        cast(on_g, 3, 0, 128)
+        cast(on_s, 3, 128, 384)
+        cast(on_s, 3, 384, 480)
+        cast(on_v, 3, 480, 896)
         cast(on_s, 3, 896, 1024)
         gather(2, 384, S)
-        planes(1, 0, 512)
-        for a, b in LAST_SLICES:
-            bank(0, a, b)
-            product(0, 0, a, b)
-        for a, b in ROW1_SLICES:
-            bank(1, a, b)
-            product(1, 0, a, b)
-        for a, b in LAST_SLICES:
+
+        slices = [[(a, a + width) for a in range(0, S, width)] for width in (SLICE, 2 * SLICE)]
+        banks = {(m, a): psum.tile([P, b - a], F32, name="bank%d_%d" % (m, a)) for m in range(2) for a, b in slices[m]}
+        y = [sb.tile([P, S], F32, name="y%d" % m) for m in range(2)]
+
+        def product(m, g, a, b):
+            cols = slice(m * P, (m + 1) * P)
+            nc.tensor.matmul_mx(
+                out=banks[m, a][:],
+                lhsT=w_words[:, g, cols].bitcast(FP8X4),
+                lhsT_scale=w_scales[:, g, cols],
+                rhs=codes[g][:, a:b].bitcast(FP8X4),
+                rhs_scale=scales[g][:, a:b],
+                start=(g == 0),
+                stop=(g == PASSES - 1),
+            )
+
+        for m in range(2):
+            for a, b in slices[m]:
+                product(m, 0, a, b)
+        woven1 = {}
+        for a, b in slices[0]:
             gather(3, a, b)
-            room(1, a, b)
-            weave(on_s, 1, a, b)
-        for a, b in LAST_SLICES:
-            quantize(1, a, b)
+            woven1[a] = sb.tile([P, 4 * SLICE], BF16, name="woven1_%d" % a, tag="woven1_%d" % a, align_bytes=64)
+            on_s(woven1[a][:].bitcast(U32).rearrange("p (s u) -> p s u", u=2), words(a, b).rearrange("p u s -> p s u"))
+        for a, b in slices[0]:
+            quantize(1, woven1[a][:], a, b)
             product(0, 1, a, b)
-            drain(on_s, 0, a, b)
-        for a, b in ROW1_SLICES:
+            on_s(y[0][:, a:b], banks[0, a][:])
+        for a, b in slices[1]:
             product(1, 1, a, b)
-            drain(on_s, 1, a, b)
+            on_s(y[1][:, a:b], banks[1, a][:])
 
         f_left = sb.tile([P, V], F32, name="f_left", tag="woven1_384", align_bytes=64)
         nc.vector.tensor_scalar(f_left[:], f_right[:], -1.0, 1.0, MULT, ADD)
@@ -222,6 +172,6 @@ def tile_picked_lerp_none_e_kernel(tc, xT, w1_words, w1_scales, frac, offs, left
             nc.vector.tensor_tensor(hi[m][:], y[m][:].indirect(right_sb[:]), f_right[:], MULT)
             nc.vector.tensor_tensor(lo[m][:], y[m][:].indirect(left_sb[:]), f_left[:], MULT)
         for m in range(2):
-            res = sb.tile([P, V], F32, name="res%d" % m, tag=("woven1_384", "res1")[m], align_bytes=64)
+            res = sb.tile([P, V], F32, name="res%d" % m, tag=("f_right", "res1")[m])
             nc.vector.tensor_tensor(res[:], lo[m][:], hi[m][:], ADD)
             nc.sync.dma_start(out[m * P : (m + 1) * P, :], res[:])

@@ -14,13 +14,13 @@ U8 = mybir.dt.uint8
 FP8X4 = mybir.dt.float8_e4m3fn_x4
 MULT = mybir.AluOpType.mult
 ADD = mybir.AluOpType.add
+COPY = mybir.ActivationFunctionType.Copy
 
 P = 128
 PASSES = 2
 SLICE = 128
-CUTS = {1: (512,), 2: (384,), 3: (384, 896)}
-FRONT = {1: 0, 2: 496, 3: 0}
-LATE = 144
+SLICES = S // SLICE
+ON_VECTOR = (448, 384, 128, 192, 0, 192)
 
 
 def tile_picked_lerp_none_e_kernel(tc, xT, w1_words, w1_scales, frac, offs, left, right, out):
@@ -34,19 +34,14 @@ def tile_picked_lerp_none_e_kernel(tc, xT, w1_words, w1_scales, frac, offs, left
         left_sb = lists.tile([P, V // 16], U16, name="left_sb")
         right_sb = lists.tile([P, V // 16], U16, name="right_sb")
 
-        x_runs = xT.rearrange("(g p u e) t -> g u p (e t)", g=PASSES, u=2, e=2)
-        rows = [sb.tile([P, T], F32, name="row%d" % e, tag="row%d" % e, align_bytes=64) for e in range(2)]
-        nc.sync.dma_start(rows[0][:], x_runs[0, 0][:, 0:T])
+        x_rows = xT.rearrange("(g p j) t -> g j p t", g=PASSES, j=4)
+        rows = [sb.tile([P, T], F32, name="row%d" % r, align_bytes=64) for r in range(8)]
+        nc.sync.dma_start(rows[0][:], x_rows[0, 0])
         nc.sync.dma_start(offs_sb[:], offs)
-        nc.sync.dma_start(rows[1][:], x_runs[0, 0][:, T : 2 * T])
-        runs = {}
-        for i in (1, 2, 3):
-            runs[i] = sb.tile([P, FRONT[i] + 2 * T], F32, name="run%d" % i, align_bytes=64)
-            ends = [0] + [T + frames for frames in CUTS[i]] + [2 * T]
-            for a, b in zip(ends, ends[1:]):
-                nc.sync.dma_start(runs[i][:, FRONT[i] + a : FRONT[i] + b], x_runs[i // 2, i % 2][:, a:b])
+        for r in range(1, 7):
+            nc.sync.dma_start(rows[r][:], x_rows[r // 4, r % 4])
 
-        w_words = sb.tile([P, PASSES, N], U32, name="w_words", align_bytes=64)
+        w_words = [sb.tile([P, N], U32, name="w_words%d" % g, align_bytes=64) for g in range(PASSES)]
         w_scales = sb.tile([P, PASSES, N], U8, name="w_scales", align_bytes=64)
         f_right = sb.tile([P, V], F32, name="f_right", tag="f_right")
         nc.gpsimd.memset(w_scales[:].rearrange("p g n -> p (g n)").bitcast(I32), 0)
@@ -55,123 +50,103 @@ def tile_picked_lerp_none_e_kernel(tc, xT, w1_words, w1_scales, frac, offs, left
                 w_scales[32 * q : 32 * q + 4, :, :].bitcast(I32),
                 w1_scales[:, 4 * q : 4 * q + 4, :].rearrange("g r n -> r g n").bitcast(I32),
             )
-        nc.sync.dma_start(w_words[:].bitcast(I32), w1_words.rearrange("g p n t -> p g (n t)").bitcast(I32))
+        w_dram = w1_words.rearrange("g p n t -> g p (n t)").bitcast(I32)
+        nc.sync.dma_start(w_words[0][:].bitcast(I32), w_dram[0])
+        nc.sync.dma_start(rows[7][:], x_rows[1, 3])
+        nc.sync.dma_start(w_words[1][:].bitcast(I32), w_dram[1])
         nc.sync.dma_start(f_right[:], frac)
         nc.sync.dma_start(right_sb[:], right)
         nc.sync.dma_start(left_sb[:], left)
 
-        on_s = nc.scalar.copy
-        on_v = nc.vector.tensor_copy
-
-        def on_g(dst, src):
-            nc.gpsimd.tensor_scalar(dst, src, 1.0, 0.0, MULT, ADD)
-
         def entries(a, b):
             return offs_sb[:, a // 16 : b // 16]
 
-        pairs = {}
+        def on_s(dst, window, offsets):
+            nc.scalar.activation(dst, window.indirect(offsets), COPY)
 
-        def cast(copy, i, a, b):
-            copy(pairs[i][:].rearrange("p (t e) -> p t e", e=2)[:, a:b, :], runs[i][:, FRONT[i] :].rearrange("p (e t) -> p t e", e=2)[:, a:b, :])
+        def on_v(dst, window, offsets):
+            nc.vector.tensor_copy(dst, window.indirect(offsets))
 
-        kept = sb.tile([P, 2, S], F32, name="kept", align_bytes=64)
-        woven0 = sb.tile([P, 2 * S], BF16, name="woven0", align_bytes=64)
-        woven0_late = runs[2][:, 0:512]
-        halves = sb.tile([P, 2, 256], U32, name="halves", align_bytes=64)
+        picked = [sb.tile([P, 2, S], F32, name="picked%d" % u, align_bytes=64) for u in range(4)]
+        woven0 = sb.tile([P, 4 * S], BF16, name="woven0", align_bytes=64)
+        woven1 = [sb.tile([P, 4 * SLICE], BF16, name="woven1_%d" % i, tag="woven1_%d" % i, align_bytes=64) for i in range(SLICES)]
         codes = [sb.tile([P, S], U32, name="codes%d" % g, align_bytes=64) for g in range(PASSES)]
         scales = [sb.tile([P, S], U8, name="scales%d" % g, align_bytes=64) for g in range(PASSES)]
+
+        def gather(engine, r, a, b):
+            engine(picked[r // 2][:, r % 2, a:b], rows[r][:], entries(a, b))
+
+        def place(dst, u, a, b):
+            nc.vector.tensor_copy(
+                dst.rearrange("p (s j) -> p s j", j=4)[:, :, 2 * (u % 2) : 2 * (u % 2) + 2],
+                picked[u][:].rearrange("p e s -> p s e")[:, a:b, :],
+            )
+
+        def gather_into_place(r):
+            on_v(woven1[0][:].rearrange("p (s j) -> p j s", j=4)[:, r % 4, :], rows[r][:], entries(0, SLICE))
 
         def quantize(g, values, a, b):
             nc.vector.quantize_mx(out=codes[g][:, a:b].bitcast(FP8X4), scales=scales[g][:, a:b], in_=values)
 
-        def keep(e, a, b):
-            on_v(kept[:, e, a:b], rows[e][:].indirect(entries(a, b)))
+        for r in range(6):
+            if ON_VECTOR[r]:
+                gather(on_v, r, 0, ON_VECTOR[r])
+            gather(on_s, r, ON_VECTOR[r], S)
+            if r in (1, 3):
+                place(woven0[:], r // 2, 0, S)
+            if r == 3:
+                quantize(0, woven0[:], 0, S)
+        for i in range(SLICES):
+            place(woven1[i][:], 2, i * SLICE, (i + 1) * SLICE)
+        gather_into_place(6)
+        gather(on_s, 6, SLICE, S)
 
-        def place(a, b):
-            on_s(woven0[:].rearrange("p (s t) -> p s t", t=4)[:, a:b, 0:2], kept[:].rearrange("p e s -> p s e")[:, a:b, :])
-
-        def gather_into_place(a, b):
-            on_v(woven0[:].bitcast(U32).rearrange("p (s u) -> p u s", u=2)[:, 1, a:b], pairs[1][:].bitcast(U32).indirect(entries(a, b)))
-
-        picked = sb.tile([P, 2, S], U32, name="picked", align_bytes=64)
-        late = runs[3][:, LATE : LATE + 2 * SLICE].bitcast(U32).rearrange("p (u s) -> p u s", u=2)
-
-        def words(a, b):
-            return late if a == S - SLICE else picked[:, :, a:b]
-
-        def gather(i, a, b):
-            on_v(words(a, b)[:, i % 2, :], pairs[i][:].bitcast(U32).indirect(entries(a, b)))
-
-        for i in (2, 3):
-            pairs[i] = sb.tile([P, 2 * T], BF16, name="pairs%d" % i, align_bytes=64)
-
-        keep(0, 0, S)
-        keep(1, 0, 256)
-        place(0, 256)
-        keep(1, 256, S)
-        on_s(halves[:, 0, :].bitcast(BF16).rearrange("p (s e) -> p s e", e=2), kept[:].rearrange("p e s -> p s e")[:, 256:S, :])
-        pairs[1] = sb.tile([P, 2 * T], BF16, name="pairs1", tag="row0", align_bytes=64)
-        cast(on_v, 1, 0, 512)
-        cast(on_v, 1, 512, 928)
-        cast(on_s, 1, 928, 1024)
-        gather_into_place(0, 256)
-        on_v(halves[:, 1, :], pairs[1][:].bitcast(U32).indirect(entries(256, S)))
-        quantize(0, woven0[:], 0, 256)
-        cast(on_s, 2, 0, 144)
-        on_v(woven0_late.bitcast(I32).rearrange("p (s u) -> p s u", u=2), halves[:].bitcast(I32).rearrange("p u s -> p s u"))
-        cast(on_g, 2, 304, 384)
-        cast(on_s, 2, 144, 304)
-        cast(on_v, 2, 768, 1024)
-        cast(on_s, 2, 384, 768)
-        quantize(0, woven0_late.bitcast(BF16), 256, S)
-        gather(2, 0, 384)
-        cast(on_g, 3, 0, 128)
-        cast(on_s, 3, 128, 384)
-        cast(on_s, 3, 384, 480)
-        cast(on_v, 3, 480, 896)
-        cast(on_s, 3, 896, 1024)
-        gather(2, 384, S)
-
-        slices = [[(a, a + width) for a in range(0, S, width)] for width in (SLICE, 2 * SLICE)]
-        banks = {(m, a): psum.tile([P, b - a], F32, name="bank%d_%d" % (m, a)) for m in range(2) for a, b in slices[m]}
+        banks = {(m, i): psum.tile([P, SLICE], F32, name="bank%d_%d" % (m, i)) for m in range(2) for i in range(SLICES)}
         y = [sb.tile([P, S], F32, name="y%d" % m) for m in range(2)]
 
-        def product(m, g, a, b):
+        def product(m, g, i):
             cols = slice(m * P, (m + 1) * P)
+            span = slice(i * SLICE, (i + 1) * SLICE)
             nc.tensor.matmul_mx(
-                out=banks[m, a][:],
-                lhsT=w_words[:, g, cols].bitcast(FP8X4),
+                out=banks[m, i][:],
+                lhsT=w_words[g][:, cols].bitcast(FP8X4),
                 lhsT_scale=w_scales[:, g, cols],
-                rhs=codes[g][:, a:b].bitcast(FP8X4),
-                rhs_scale=scales[g][:, a:b],
+                rhs=codes[g][:, span].bitcast(FP8X4),
+                rhs_scale=scales[g][:, span],
                 start=(g == 0),
                 stop=(g == PASSES - 1),
             )
 
-        for m in range(2):
-            for a, b in slices[m]:
-                product(m, 0, a, b)
-        woven1 = {}
-        for a, b in slices[0]:
-            gather(3, a, b)
-            woven1[a] = sb.tile([P, 4 * SLICE], BF16, name="woven1_%d" % a, tag="woven1_%d" % a, align_bytes=64)
-            on_s(woven1[a][:].bitcast(U32).rearrange("p (s u) -> p s u", u=2), words(a, b).rearrange("p u s -> p s u"))
-        for a, b in slices[0]:
-            quantize(1, woven1[a][:], a, b)
-            product(0, 1, a, b)
-            on_s(y[0][:, a:b], banks[0, a][:])
-        for a, b in slices[1]:
-            product(1, 1, a, b)
-            on_s(y[1][:, a:b], banks[1, a][:])
+        for i in range(SLICES):
+            for m in range(2):
+                product(m, 0, i)
 
-        f_left = sb.tile([P, V], F32, name="f_left", tag="woven1_384", align_bytes=64)
-        nc.vector.tensor_scalar(f_left[:], f_right[:], -1.0, 1.0, MULT, ADD)
+        gather_into_place(7)
+        for i in range(1, SLICES):
+            gather(on_s, 7, i * SLICE, (i + 1) * SLICE)
+        for i in range(SLICES):
+            if i + 1 < SLICES:
+                place(woven1[i + 1][:], 3, (i + 1) * SLICE, (i + 2) * SLICE)
+            quantize(1, woven1[i][:], i * SLICE, (i + 1) * SLICE)
+            for m in range(2):
+                product(m, 1, i)
+        for i in range(SLICES):
+            if i == SLICES - 2:
+                f_left = sb.tile([P, V], F32, name="f_left", tag="woven1_%d" % (SLICES - 1), align_bytes=64)
+                nc.vector.tensor_scalar(f_left[:], f_right[:], -1.0, 1.0, MULT, ADD)
+            for m in range(2):
+                copy = nc.vector.tensor_copy if i == SLICES - 2 else nc.scalar.copy
+                copy(y[m][:, i * SLICE : (i + 1) * SLICE], banks[m, i][:])
+
         lo = [sb.tile([P, V], F32, name="lo%d" % m) for m in range(2)]
         hi = [sb.tile([P, V], F32, name="hi%d" % m) for m in range(2)]
+        at_left = [sb.tile([P, V], F32, name="at_left%d" % m) for m in range(2)]
+        res = [sb.tile([P, V], F32, name="res%d" % m) for m in range(2)]
         for m in range(2):
+            on_s(at_left[m][:], y[m][:], left_sb[:])
             nc.vector.tensor_tensor(hi[m][:], y[m][:].indirect(right_sb[:]), f_right[:], MULT)
-            nc.vector.tensor_tensor(lo[m][:], y[m][:].indirect(left_sb[:]), f_left[:], MULT)
         for m in range(2):
-            res = sb.tile([P, V], F32, name="res%d" % m, tag=("f_right", "res1")[m])
-            nc.vector.tensor_tensor(res[:], lo[m][:], hi[m][:], ADD)
-            nc.sync.dma_start(out[m * P : (m + 1) * P, :], res[:])
+            nc.vector.tensor_tensor(lo[m][:], at_left[m][:], f_left[:], MULT)
+        for m in range(2):
+            nc.vector.tensor_tensor(res[m][:], lo[m][:], hi[m][:], ADD)
+            nc.sync.dma_start(out[m * P : (m + 1) * P, :], res[m][:])

@@ -20,7 +20,8 @@ P = 128
 PASSES = 2
 SLICE = 128
 SLICES = S // SLICE
-ON_VECTOR = (448, 384, 128, 192, 0, 192)
+OWN = (2 * SLICE, SLICE)
+FIRST_ON_SCALAR = 64
 
 
 def tile_picked_lerp_none_e_kernel(tc, xT, w1_words, w1_scales, frac, offs, left, right, out):
@@ -41,7 +42,9 @@ def tile_picked_lerp_none_e_kernel(tc, xT, w1_words, w1_scales, frac, offs, left
         for r in range(1, 7):
             nc.sync.dma_start(rows[r][:], x_rows[r // 4, r % 4])
 
-        w_words = [sb.tile([P, N], U32, name="w_words%d" % g, align_bytes=64) for g in range(PASSES)]
+        w_first = [sb.tile([P, P], U32, name="w_first%d" % m, align_bytes=64) for m in range(2)]
+        w_second = sb.tile([P, N], U32, name="w_second", align_bytes=64)
+        w_words = {(0, 0): w_first[0][:], (0, 1): w_first[1][:], (1, 0): w_second[:, 0:P], (1, 1): w_second[:, P:N]}
         w_scales = sb.tile([P, PASSES, N], U8, name="w_scales", align_bytes=64)
         f_right = sb.tile([P, V], F32, name="f_right", tag="f_right")
         nc.gpsimd.memset(w_scales[:].rearrange("p g n -> p (g n)").bitcast(I32), 0)
@@ -51,9 +54,10 @@ def tile_picked_lerp_none_e_kernel(tc, xT, w1_words, w1_scales, frac, offs, left
                 w1_scales[:, 4 * q : 4 * q + 4, :].rearrange("g r n -> r g n").bitcast(I32),
             )
         w_dram = w1_words.rearrange("g p n t -> g p (n t)").bitcast(I32)
-        nc.sync.dma_start(w_words[0][:].bitcast(I32), w_dram[0])
+        nc.sync.dma_start(w_first[0][:].bitcast(I32), w_dram[0][:, 0:P])
         nc.sync.dma_start(rows[7][:], x_rows[1, 3])
-        nc.sync.dma_start(w_words[1][:].bitcast(I32), w_dram[1])
+        nc.sync.dma_start(w_first[1][:].bitcast(I32), w_dram[0][:, P:N])
+        nc.sync.dma_start(w_second[:].bitcast(I32), w_dram[1])
         nc.sync.dma_start(f_right[:], frac)
         nc.sync.dma_start(right_sb[:], right)
         nc.sync.dma_start(left_sb[:], left)
@@ -67,39 +71,44 @@ def tile_picked_lerp_none_e_kernel(tc, xT, w1_words, w1_scales, frac, offs, left
         def on_v(dst, window, offsets):
             nc.vector.tensor_copy(dst, window.indirect(offsets))
 
-        picked = [sb.tile([P, 2, S], F32, name="picked%d" % u, align_bytes=64) for u in range(4)]
-        woven0 = sb.tile([P, 4 * S], BF16, name="woven0", align_bytes=64)
-        woven1 = [sb.tile([P, 4 * SLICE], BF16, name="woven1_%d" % i, tag="woven1_%d" % i, align_bytes=64) for i in range(SLICES)]
+        picked = [sb.tile([P, 4, S - OWN[g]], F32, name="picked%d" % g, align_bytes=64) for g in range(PASSES)]
+        own = [sb.tile([P, 4 * OWN[g]], BF16, name="own%d" % g, align_bytes=64) for g in range(PASSES)]
+        rest = [sb.tile([P, 4 * (S - OWN[g])], BF16, name="rest%d" % g, tag="rest%d" % g, align_bytes=64) for g in range(PASSES)]
         codes = [sb.tile([P, S], U32, name="codes%d" % g, align_bytes=64) for g in range(PASSES)]
         scales = [sb.tile([P, S], U8, name="scales%d" % g, align_bytes=64) for g in range(PASSES)]
 
-        def gather(engine, r, a, b):
-            engine(picked[r // 2][:, r % 2, a:b], rows[r][:], entries(a, b))
+        def gather_into_place(r):
+            on_v(own[r // 4][:].rearrange("p (s j) -> p j s", j=4)[:, r % 4, :], rows[r][:], entries(0, OWN[r // 4]))
 
-        def place(dst, u, a, b):
+        def gather(engine, r, a, b):
+            first = OWN[r // 4]
+            engine(picked[r // 4][:, r % 4, a - first : b - first], rows[r][:], entries(a, b))
+
+        def place(g, j0, j1, a, b):
+            first = OWN[g]
             nc.vector.tensor_copy(
-                dst.rearrange("p (s j) -> p s j", j=4)[:, :, 2 * (u % 2) : 2 * (u % 2) + 2],
-                picked[u][:].rearrange("p e s -> p s e")[:, a:b, :],
+                rest[g][:].rearrange("p (s j) -> p s j", j=4)[:, a - first : b - first, j0:j1],
+                picked[g][:].rearrange("p j s -> p s j")[:, a - first : b - first, j0:j1],
             )
 
-        def gather_into_place(r):
-            on_v(woven1[0][:].rearrange("p (s j) -> p j s", j=4)[:, r % 4, :], rows[r][:], entries(0, SLICE))
-
-        def quantize(g, values, a, b):
+        def quantize(g, a, b):
+            values = own[g][:, 4 * a : 4 * b] if a < OWN[g] else rest[g][:, 4 * (a - OWN[g]) : 4 * (b - OWN[g])]
             nc.vector.quantize_mx(out=codes[g][:, a:b].bitcast(FP8X4), scales=scales[g][:, a:b], in_=values)
 
-        for r in range(6):
-            if ON_VECTOR[r]:
-                gather(on_v, r, 0, ON_VECTOR[r])
-            gather(on_s, r, ON_VECTOR[r], S)
-            if r in (1, 3):
-                place(woven0[:], r // 2, 0, S)
-            if r == 3:
-                quantize(0, woven0[:], 0, S)
-        for i in range(SLICES):
-            place(woven1[i][:], 2, i * SLICE, (i + 1) * SLICE)
-        gather_into_place(6)
-        gather(on_s, 6, SLICE, S)
+        gather_into_place(0)
+        gather(on_v, 0, OWN[0], S - FIRST_ON_SCALAR)
+        gather(on_s, 0, S - FIRST_ON_SCALAR, S)
+        for r in range(1, 4):
+            gather_into_place(r)
+            gather(on_s, r, OWN[0], S)
+        place(0, 0, 4, OWN[0], S)
+        quantize(0, 0, OWN[0])
+        quantize(0, OWN[0], S)
+        for r in range(4, 7):
+            gather_into_place(r)
+            gather(on_s, r, OWN[1], S)
+            if r == 5:
+                place(1, 0, 2, OWN[1], S)
 
         banks = {(m, i): psum.tile([P, SLICE], F32, name="bank%d_%d" % (m, i)) for m in range(2) for i in range(SLICES)}
         y = [sb.tile([P, S], F32, name="y%d" % m) for m in range(2)]
@@ -109,7 +118,7 @@ def tile_picked_lerp_none_e_kernel(tc, xT, w1_words, w1_scales, frac, offs, left
             span = slice(i * SLICE, (i + 1) * SLICE)
             nc.tensor.matmul_mx(
                 out=banks[m, i][:],
-                lhsT=w_words[g][:, cols].bitcast(FP8X4),
+                lhsT=w_words[g, m].bitcast(FP8X4),
                 lhsT_scale=w_scales[:, g, cols],
                 rhs=codes[g][:, span].bitcast(FP8X4),
                 rhs_scale=scales[g][:, span],
@@ -117,8 +126,8 @@ def tile_picked_lerp_none_e_kernel(tc, xT, w1_words, w1_scales, frac, offs, left
                 stop=(g == PASSES - 1),
             )
 
-        for i in range(SLICES):
-            for m in range(2):
+        for m in range(2):
+            for i in range(SLICES):
                 product(m, 0, i)
 
         gather_into_place(7)
@@ -126,17 +135,16 @@ def tile_picked_lerp_none_e_kernel(tc, xT, w1_words, w1_scales, frac, offs, left
             gather(on_s, 7, i * SLICE, (i + 1) * SLICE)
         for i in range(SLICES):
             if i + 1 < SLICES:
-                place(woven1[i + 1][:], 3, (i + 1) * SLICE, (i + 2) * SLICE)
-            quantize(1, woven1[i][:], i * SLICE, (i + 1) * SLICE)
+                place(1, 2, 4, (i + 1) * SLICE, (i + 2) * SLICE)
+            quantize(1, i * SLICE, (i + 1) * SLICE)
             for m in range(2):
                 product(m, 1, i)
         for i in range(SLICES):
-            if i == SLICES - 2:
-                f_left = sb.tile([P, V], F32, name="f_left", tag="woven1_%d" % (SLICES - 1), align_bytes=64)
-                nc.vector.tensor_scalar(f_left[:], f_right[:], -1.0, 1.0, MULT, ADD)
             for m in range(2):
                 copy = nc.vector.tensor_copy if i == SLICES - 2 else nc.scalar.copy
                 copy(y[m][:, i * SLICE : (i + 1) * SLICE], banks[m, i][:])
+        f_left = sb.tile([P, V], F32, name="f_left", tag="rest1", align_bytes=64)
+        nc.vector.tensor_scalar(f_left[:], f_right[:], -1.0, 1.0, MULT, ADD)
 
         lo = [sb.tile([P, V], F32, name="lo%d" % m) for m in range(2)]
         hi = [sb.tile([P, V], F32, name="hi%d" % m) for m in range(2)]

@@ -42,9 +42,7 @@ def tile_picked_lerp_none_e_kernel(tc, xT, w1_words, w1_scales, frac, offs, left
         for r in range(1, 7):
             nc.sync.dma_start(rows[r][:], x_rows[r // 4, r % 4])
 
-        w_first = [sb.tile([P, P], U32, name="w_first%d" % m, align_bytes=64) for m in range(2)]
-        w_second = sb.tile([P, N], U32, name="w_second", align_bytes=64)
-        w_words = {(0, 0): w_first[0][:], (0, 1): w_first[1][:], (1, 0): w_second[:, 0:P], (1, 1): w_second[:, P:N]}
+        w_words = [sb.tile([P, N], U32, name="w_words%d" % g, align_bytes=64) for g in range(PASSES)]
         w_scales = sb.tile([P, PASSES, N], U8, name="w_scales", align_bytes=64)
         f_right = sb.tile([P, V], F32, name="f_right", tag="f_right")
         nc.gpsimd.memset(w_scales[:].rearrange("p g n -> p (g n)").bitcast(I32), 0)
@@ -54,10 +52,9 @@ def tile_picked_lerp_none_e_kernel(tc, xT, w1_words, w1_scales, frac, offs, left
                 w1_scales[:, 4 * q : 4 * q + 4, :].rearrange("g r n -> r g n").bitcast(I32),
             )
         w_dram = w1_words.rearrange("g p n t -> g p (n t)").bitcast(I32)
-        nc.sync.dma_start(w_first[0][:].bitcast(I32), w_dram[0][:, 0:P])
+        nc.sync.dma_start(w_words[0][:].bitcast(I32), w_dram[0])
         nc.sync.dma_start(rows[7][:], x_rows[1, 3])
-        nc.sync.dma_start(w_first[1][:].bitcast(I32), w_dram[0][:, P:N])
-        nc.sync.dma_start(w_second[:].bitcast(I32), w_dram[1])
+        nc.sync.dma_start(w_words[1][:].bitcast(I32), w_dram[1])
         nc.sync.dma_start(f_right[:], frac)
         nc.sync.dma_start(right_sb[:], right)
         nc.sync.dma_start(left_sb[:], left)
@@ -118,7 +115,7 @@ def tile_picked_lerp_none_e_kernel(tc, xT, w1_words, w1_scales, frac, offs, left
             span = slice(i * SLICE, (i + 1) * SLICE)
             nc.tensor.matmul_mx(
                 out=banks[m, i][:],
-                lhsT=w_words[g, m].bitcast(FP8X4),
+                lhsT=w_words[g][:, cols].bitcast(FP8X4),
                 lhsT_scale=w_scales[:, g, cols],
                 rhs=codes[g][:, span].bitcast(FP8X4),
                 rhs_scale=scales[g][:, span],

@@ -20,8 +20,7 @@ P = 128
 PASSES = 2
 SLICE = 128
 SLICES = S // SLICE
-OWN = (2 * SLICE, SLICE)
-FIRST_ON_SCALAR = 64
+ON_VECTOR = (448, 384, 0, 256)
 
 
 def tile_picked_lerp_none_e_kernel(tc, xT, w1_words, w1_scales, frac, offs, left, right, out):
@@ -68,44 +67,41 @@ def tile_picked_lerp_none_e_kernel(tc, xT, w1_words, w1_scales, frac, offs, left
         def on_v(dst, window, offsets):
             nc.vector.tensor_copy(dst, window.indirect(offsets))
 
-        picked = [sb.tile([P, 4, S - OWN[g]], F32, name="picked%d" % g, align_bytes=64) for g in range(PASSES)]
-        own = [sb.tile([P, 4 * OWN[g]], BF16, name="own%d" % g, align_bytes=64) for g in range(PASSES)]
-        rest = [sb.tile([P, 4 * (S - OWN[g])], BF16, name="rest%d" % g, tag="rest%d" % g, align_bytes=64) for g in range(PASSES)]
+        picked = [sb.tile([P, 2, S], F32, name="picked%d" % u, align_bytes=64) for u in range(4)]
+        woven = [sb.tile([P, 4 * S], BF16, name="woven%d" % g, tag="woven%d" % g, align_bytes=64) for g in range(PASSES)]
         codes = [sb.tile([P, S], U32, name="codes%d" % g, align_bytes=64) for g in range(PASSES)]
         scales = [sb.tile([P, S], U8, name="scales%d" % g, align_bytes=64) for g in range(PASSES)]
 
         def gather_into_place(r):
-            on_v(own[r // 4][:].rearrange("p (s j) -> p j s", j=4)[:, r % 4, :], rows[r][:], entries(0, OWN[r // 4]))
+            on_v(woven[r // 4][:].rearrange("p (s j) -> p j s", j=4)[:, r % 4, 0:SLICE], rows[r][:], entries(0, SLICE))
 
         def gather(engine, r, a, b):
-            first = OWN[r // 4]
-            engine(picked[r // 4][:, r % 4, a - first : b - first], rows[r][:], entries(a, b))
+            engine(picked[r // 2][:, r % 2, a:b], rows[r][:], entries(a, b))
 
-        def place(g, j0, j1, a, b):
-            first = OWN[g]
+        def place(u, a, b):
             nc.vector.tensor_copy(
-                rest[g][:].rearrange("p (s j) -> p s j", j=4)[:, a - first : b - first, j0:j1],
-                picked[g][:].rearrange("p j s -> p s j")[:, a - first : b - first, j0:j1],
+                woven[u // 2][:].rearrange("p (s j) -> p s j", j=4)[:, a:b, 2 * (u % 2) : 2 * (u % 2) + 2],
+                picked[u][:].rearrange("p e s -> p s e")[:, a:b, :],
             )
 
         def quantize(g, a, b):
-            values = own[g][:, 4 * a : 4 * b] if a < OWN[g] else rest[g][:, 4 * (a - OWN[g]) : 4 * (b - OWN[g])]
-            nc.vector.quantize_mx(out=codes[g][:, a:b].bitcast(FP8X4), scales=scales[g][:, a:b], in_=values)
+            nc.vector.quantize_mx(out=codes[g][:, a:b].bitcast(FP8X4), scales=scales[g][:, a:b], in_=woven[g][:, 4 * a : 4 * b])
 
-        gather_into_place(0)
-        gather(on_v, 0, OWN[0], S - FIRST_ON_SCALAR)
-        gather(on_s, 0, S - FIRST_ON_SCALAR, S)
-        for r in range(1, 4):
-            gather_into_place(r)
-            gather(on_s, r, OWN[0], S)
-        place(0, 0, 4, OWN[0], S)
-        quantize(0, 0, OWN[0])
-        quantize(0, OWN[0], S)
-        for r in range(4, 7):
-            gather_into_place(r)
-            gather(on_s, r, OWN[1], S)
-            if r == 5:
-                place(1, 0, 2, OWN[1], S)
+        for r in range(4):
+            if ON_VECTOR[r]:
+                gather(on_v, r, 0, ON_VECTOR[r])
+            gather(on_s, r, ON_VECTOR[r], S)
+            if r % 2 == 1:
+                place(r // 2, 0, S)
+        quantize(0, 0, S)
+        gather(on_s, 4, 0, S)
+        gather(on_s, 5, 2 * SLICE, S)
+        gather(on_v, 5, SLICE, 2 * SLICE)
+        gather(on_s, 5, 0, SLICE)
+        place(2, 2 * SLICE, S)
+        gather_into_place(6)
+        gather(on_s, 6, SLICE, S)
+        place(2, 0, 2 * SLICE)
 
         banks = {(m, i): psum.tile([P, SLICE], F32, name="bank%d_%d" % (m, i)) for m in range(2) for i in range(SLICES)}
         y = [sb.tile([P, S], F32, name="y%d" % m) for m in range(2)]
@@ -132,7 +128,7 @@ def tile_picked_lerp_none_e_kernel(tc, xT, w1_words, w1_scales, frac, offs, left
             gather(on_s, 7, i * SLICE, (i + 1) * SLICE)
         for i in range(SLICES):
             if i + 1 < SLICES:
-                place(1, 2, 4, (i + 1) * SLICE, (i + 2) * SLICE)
+                place(3, (i + 1) * SLICE, (i + 2) * SLICE)
             quantize(1, i * SLICE, (i + 1) * SLICE)
             for m in range(2):
                 product(m, 1, i)
@@ -140,7 +136,7 @@ def tile_picked_lerp_none_e_kernel(tc, xT, w1_words, w1_scales, frac, offs, left
             for m in range(2):
                 copy = nc.vector.tensor_copy if i == SLICES - 2 else nc.scalar.copy
                 copy(y[m][:, i * SLICE : (i + 1) * SLICE], banks[m, i][:])
-        f_left = sb.tile([P, V], F32, name="f_left", tag="rest1", align_bytes=64)
+        f_left = sb.tile([P, V], F32, name="f_left", tag="woven1", align_bytes=64)
         nc.vector.tensor_scalar(f_left[:], f_right[:], -1.0, 1.0, MULT, ADD)
 
         lo = [sb.tile([P, V], F32, name="lo%d" % m) for m in range(2)]

@@ -20,7 +20,8 @@ P = 128
 PASSES = 2
 SLICE = 128
 SLICES = S // SLICE
-ON_VECTOR = (448, 384, 0, 256)
+AHEAD = 2
+ON_VECTOR = (448, 512, 0, 256, 0)
 
 
 def tile_picked_lerp_none_e_kernel(tc, xT, w1_words, w1_scales, frac, offs, left, right, out):
@@ -51,8 +52,8 @@ def tile_picked_lerp_none_e_kernel(tc, xT, w1_words, w1_scales, frac, offs, left
                 w1_scales[:, 4 * q : 4 * q + 4, :].rearrange("g r n -> r g n").bitcast(I32),
             )
         w_dram = w1_words.rearrange("g p n t -> g p (n t)").bitcast(I32)
-        nc.sync.dma_start(w_words[0][:].bitcast(I32), w_dram[0])
         nc.sync.dma_start(rows[7][:], x_rows[1, 3])
+        nc.sync.dma_start(w_words[0][:].bitcast(I32), w_dram[0])
         nc.sync.dma_start(w_words[1][:].bitcast(I32), w_dram[1])
         nc.sync.dma_start(f_right[:], frac)
         nc.sync.dma_start(right_sb[:], right)
@@ -87,21 +88,29 @@ def tile_picked_lerp_none_e_kernel(tc, xT, w1_words, w1_scales, frac, offs, left
         def quantize(g, a, b):
             nc.vector.quantize_mx(out=codes[g][:, a:b].bitcast(FP8X4), scales=scales[g][:, a:b], in_=woven[g][:, 4 * a : 4 * b])
 
-        for r in range(4):
+        def gather_row(r):
             if ON_VECTOR[r]:
                 gather(on_v, r, 0, ON_VECTOR[r])
-            gather(on_s, r, ON_VECTOR[r], S)
-            if r % 2 == 1:
-                place(r // 2, 0, S)
-        quantize(0, 0, S)
-        gather(on_s, 4, 0, S)
+            if ON_VECTOR[r] < S:
+                gather(on_s, r, ON_VECTOR[r], S)
+
+        gather_row(0)
+        gather_row(1)
+        place(0, 0, S)
+        gather_row(2)
+        gather_row(3)
+        place(1, ON_VECTOR[3], S)
+        place(1, 0, ON_VECTOR[3])
+        quantize(0, ON_VECTOR[3], S)
+        quantize(0, 0, ON_VECTOR[3])
+        gather_row(4)
         gather(on_s, 5, 2 * SLICE, S)
         gather(on_v, 5, SLICE, 2 * SLICE)
         gather(on_s, 5, 0, SLICE)
         place(2, 2 * SLICE, S)
+        place(2, 0, 2 * SLICE)
         gather_into_place(6)
         gather(on_s, 6, SLICE, S)
-        place(2, 0, 2 * SLICE)
 
         banks = {(m, i): psum.tile([P, SLICE], F32, name="bank%d_%d" % (m, i)) for m in range(2) for i in range(SLICES)}
         y = [sb.tile([P, S], F32, name="y%d" % m) for m in range(2)]
@@ -119,8 +128,8 @@ def tile_picked_lerp_none_e_kernel(tc, xT, w1_words, w1_scales, frac, offs, left
                 stop=(g == PASSES - 1),
             )
 
-        for m in range(2):
-            for i in range(SLICES):
+        for i in range(AHEAD):
+            for m in range(2):
                 product(m, 0, i)
 
         gather_into_place(7)
@@ -130,8 +139,13 @@ def tile_picked_lerp_none_e_kernel(tc, xT, w1_words, w1_scales, frac, offs, left
             if i + 1 < SLICES:
                 place(3, (i + 1) * SLICE, (i + 2) * SLICE)
             quantize(1, i * SLICE, (i + 1) * SLICE)
-            for m in range(2):
-                product(m, 1, i)
+            product(0, 1, i)
+            if i + AHEAD < SLICES:
+                product(1, 1, i)
+                for m in range(2):
+                    product(m, 0, i + AHEAD)
+        for i in range(SLICES - AHEAD, SLICES):
+            product(1, 1, i)
         for i in range(SLICES):
             for m in range(2):
                 copy = nc.vector.tensor_copy if i == SLICES - 2 else nc.scalar.copy

@@ -19,9 +19,7 @@ COPY = mybir.ActivationFunctionType.Copy
 P = 128
 PASSES = 2
 SLICE = 128
-SLICES = S // SLICE
-AHEAD = 2
-ON_VECTOR = (448, 512, 0, 256, 0)
+HALF = 256
 
 
 def tile_picked_lerp_none_e_kernel(tc, xT, w1_words, w1_scales, frac, offs, left, right, out):
@@ -44,7 +42,7 @@ def tile_picked_lerp_none_e_kernel(tc, xT, w1_words, w1_scales, frac, offs, left
 
         w_words = [sb.tile([P, N], U32, name="w_words%d" % g, align_bytes=64) for g in range(PASSES)]
         w_scales = sb.tile([P, PASSES, N], U8, name="w_scales", align_bytes=64)
-        f_right = sb.tile([P, V], F32, name="f_right", tag="f_right")
+        f_right = sb.tile([P, V], F32, name="f_right")
         nc.gpsimd.memset(w_scales[:].rearrange("p g n -> p (g n)").bitcast(I32), 0)
         for q in range(4):
             nc.sync.dma_start(
@@ -59,8 +57,10 @@ def tile_picked_lerp_none_e_kernel(tc, xT, w1_words, w1_scales, frac, offs, left
         nc.sync.dma_start(right_sb[:], right)
         nc.sync.dma_start(left_sb[:], left)
 
-        def entries(a, b):
-            return offs_sb[:, a // 16 : b // 16]
+        picked = [sb.tile([P, 2, S], F32, name="picked%d" % u, align_bytes=64) for u in range(4)]
+        woven = [sb.tile([P, 4 * S], BF16, name="woven%d" % g, tag="woven%d" % g, align_bytes=64) for g in range(PASSES)]
+        codes = [sb.tile([P, S], U32, name="codes%d" % g, align_bytes=64) for g in range(PASSES)]
+        scales = [sb.tile([P, S], U8, name="scales%d" % g, align_bytes=64) for g in range(PASSES)]
 
         def on_s(dst, window, offsets):
             nc.scalar.activation(dst, window.indirect(offsets), COPY)
@@ -68,90 +68,94 @@ def tile_picked_lerp_none_e_kernel(tc, xT, w1_words, w1_scales, frac, offs, left
         def on_v(dst, window, offsets):
             nc.vector.tensor_copy(dst, window.indirect(offsets))
 
-        picked = [sb.tile([P, 2, S], F32, name="picked%d" % u, align_bytes=64) for u in range(4)]
-        woven = [sb.tile([P, 4 * S], BF16, name="woven%d" % g, tag="woven%d" % g, align_bytes=64) for g in range(PASSES)]
-        codes = [sb.tile([P, S], U32, name="codes%d" % g, align_bytes=64) for g in range(PASSES)]
-        scales = [sb.tile([P, S], U8, name="scales%d" % g, align_bytes=64) for g in range(PASSES)]
-
-        def gather_into_place(r):
-            on_v(woven[r // 4][:].rearrange("p (s j) -> p j s", j=4)[:, r % 4, 0:SLICE], rows[r][:], entries(0, SLICE))
-
         def gather(engine, r, a, b):
-            engine(picked[r // 2][:, r % 2, a:b], rows[r][:], entries(a, b))
+            engine(picked[r // 2][:, r % 2, a:b], rows[r][:], offs_sb[:, a // 16 : b // 16])
 
-        def place(u, a, b):
-            nc.vector.tensor_copy(
+        def gather_into_place(r, a, b):
+            on_v(woven[r // 4][:].rearrange("p (s j) -> p j s", j=4)[:, r % 4, a:b], rows[r][:], offs_sb[:, a // 16 : b // 16])
+
+        def pair_views(u, a, b):
+            return (
                 woven[u // 2][:].rearrange("p (s j) -> p s j", j=4)[:, a:b, 2 * (u % 2) : 2 * (u % 2) + 2],
                 picked[u][:].rearrange("p e s -> p s e")[:, a:b, :],
             )
 
+        def place(u, a, b):
+            nc.vector.tensor_copy(*pair_views(u, a, b))
+
         def quantize(g, a, b):
             nc.vector.quantize_mx(out=codes[g][:, a:b].bitcast(FP8X4), scales=scales[g][:, a:b], in_=woven[g][:, 4 * a : 4 * b])
 
-        def gather_row(r):
-            if ON_VECTOR[r]:
-                gather(on_v, r, 0, ON_VECTOR[r])
-            if ON_VECTOR[r] < S:
-                gather(on_s, r, ON_VECTOR[r], S)
-
-        gather_row(0)
-        gather_row(1)
+        gather(on_v, 0, 0, 448)
+        gather(on_s, 0, 448, S)
+        gather(on_v, 1, 0, S)
         place(0, 0, S)
-        gather_row(2)
-        gather_row(3)
-        place(1, ON_VECTOR[3], S)
-        place(1, 0, ON_VECTOR[3])
-        quantize(0, ON_VECTOR[3], S)
-        quantize(0, 0, ON_VECTOR[3])
-        gather_row(4)
-        gather(on_s, 5, 2 * SLICE, S)
-        gather(on_v, 5, SLICE, 2 * SLICE)
-        gather(on_s, 5, 0, SLICE)
-        place(2, 2 * SLICE, S)
-        place(2, 0, 2 * SLICE)
-        gather_into_place(6)
-        gather(on_s, 6, SLICE, S)
+        gather(on_s, 2, 0, S)
+        gather(on_v, 3, 0, HALF)
+        gather(on_s, 3, HALF, S)
+        place(1, HALF, S)
+        place(1, 0, HALF)
+        quantize(0, HALF, S)
+        quantize(0, 0, HALF)
+        gather(on_s, 4, 0, S)
+        gather(on_v, 5, 0, SLICE)
+        gather(on_s, 5, SLICE, HALF)
+        gather(on_s, 5, HALF, S)
+        place(2, 0, HALF)
+        nc.gpsimd.tensor_scalar(*pair_views(2, HALF, S), 1.0, 0.0, MULT, ADD)
+        gather_into_place(6, 0, HALF)
+        gather(on_s, 6, HALF, S)
 
-        banks = {(m, i): psum.tile([P, SLICE], F32, name="bank%d_%d" % (m, i)) for m in range(2) for i in range(SLICES)}
-        y = [sb.tile([P, S], F32, name="y%d" % m) for m in range(2)]
+        groups = [(m, i * SLICE, (i + 1) * SLICE) for m in range(2) for i in range(4)]
+        banks = {grp: psum.tile([P, grp[2] - grp[1]], F32, name="bank%d_%d" % grp[:2]) for grp in groups}
+        y = [sb.tile([P, S], F32, name="y%d" % m, tag="y%d" % m) for m in range(2)]
 
-        def product(m, g, i):
+        def product(g, grp):
+            m, a, b = grp
             cols = slice(m * P, (m + 1) * P)
-            span = slice(i * SLICE, (i + 1) * SLICE)
             nc.tensor.matmul_mx(
-                out=banks[m, i][:],
+                out=banks[grp][:],
                 lhsT=w_words[g][:, cols].bitcast(FP8X4),
                 lhsT_scale=w_scales[:, g, cols],
-                rhs=codes[g][:, span].bitcast(FP8X4),
-                rhs_scale=scales[g][:, span],
+                rhs=codes[g][:, a:b].bitcast(FP8X4),
+                rhs_scale=scales[g][:, a:b],
                 start=(g == 0),
                 stop=(g == PASSES - 1),
             )
 
-        for i in range(AHEAD):
-            for m in range(2):
-                product(m, 0, i)
+        def empty(copy, grp):
+            m, a, b = grp
+            copy(y[m][:, a:b], banks[grp][:])
 
-        gather_into_place(7)
-        for i in range(1, SLICES):
-            gather(on_s, 7, i * SLICE, (i + 1) * SLICE)
-        for i in range(SLICES):
-            if i + 1 < SLICES:
-                place(3, (i + 1) * SLICE, (i + 2) * SLICE)
+        gather_into_place(7, 0, SLICE)
+        gather_into_place(7, SLICE, HALF)
+        gather(on_s, 7, HALF, HALF + SLICE)
+        gather(on_s, 7, HALF + SLICE, S)
+        nc.gpsimd.tensor_scalar(*pair_views(3, HALF, HALF + SLICE), 1.0, 0.0, MULT, ADD)
+        nc.scalar.activation(*pair_views(3, HALF + SLICE, S), COPY)
+        for i in range(4):
             quantize(1, i * SLICE, (i + 1) * SLICE)
-            product(0, 1, i)
-            if i + AHEAD < SLICES:
-                product(1, 1, i)
-                for m in range(2):
-                    product(m, 0, i + AHEAD)
-        for i in range(SLICES - AHEAD, SLICES):
-            product(1, 1, i)
-        for i in range(SLICES):
-            for m in range(2):
-                copy = nc.vector.tensor_copy if i == SLICES - 2 else nc.scalar.copy
-                copy(y[m][:, i * SLICE : (i + 1) * SLICE], banks[m, i][:])
+
+        for grp in groups[:7]:
+            product(0, grp)
+        product(1, groups[0])
+        product(1, groups[4])
+        for grp in groups[1:4]:
+            product(1, grp)
+        product(1, groups[5])
+        product(0, groups[7])
+        product(1, groups[6])
+        product(1, groups[7])
+
+        empty(nc.scalar.copy, groups[0])
+        empty(nc.vector.tensor_copy, groups[4])
+        for grp in groups[1:4]:
+            empty(nc.scalar.copy, grp)
         f_left = sb.tile([P, V], F32, name="f_left", tag="woven1", align_bytes=64)
         nc.vector.tensor_scalar(f_left[:], f_right[:], -1.0, 1.0, MULT, ADD)
+        empty(nc.vector.tensor_copy, groups[5])
+        empty(nc.scalar.copy, groups[6])
+        empty(nc.scalar.copy, groups[7])
 
         lo = [sb.tile([P, V], F32, name="lo%d" % m) for m in range(2)]
         hi = [sb.tile([P, V], F32, name="hi%d" % m) for m in range(2)]

@@ -40,7 +40,9 @@ def tile_picked_lerp_none_e_kernel(tc, xT, w1_words, w1_scales, frac, offs, left
         for r in range(1, 7):
             nc.sync.dma_start(rows[r][:], x_rows[r // 4, r % 4])
 
-        w_words = [sb.tile([P, N], U32, name="w_words%d" % g, align_bytes=64) for g in range(PASSES)]
+        first_words = [sb.tile([P, P], U32, name="first_words%d" % m, align_bytes=64) for m in range(2)]
+        last_words = sb.tile([P, N], U32, name="last_words", align_bytes=64)
+        w_words = [[first_words[0][:], first_words[1][:]], [last_words[:, 0:P], last_words[:, P:N]]]
         w_scales = sb.tile([P, PASSES, N], U8, name="w_scales", align_bytes=64)
         f_right = sb.tile([P, V], F32, name="f_right")
         nc.gpsimd.memset(w_scales[:].rearrange("p g n -> p (g n)").bitcast(I32), 0)
@@ -51,8 +53,9 @@ def tile_picked_lerp_none_e_kernel(tc, xT, w1_words, w1_scales, frac, offs, left
             )
         w_dram = w1_words.rearrange("g p n t -> g p (n t)").bitcast(I32)
         nc.sync.dma_start(rows[7][:], x_rows[1, 3])
-        nc.sync.dma_start(w_words[0][:].bitcast(I32), w_dram[0])
-        nc.sync.dma_start(w_words[1][:].bitcast(I32), w_dram[1])
+        for m in range(2):
+            nc.sync.dma_start(first_words[m][:].bitcast(I32), w_dram[0][:, m * P : (m + 1) * P])
+        nc.sync.dma_start(last_words[:].bitcast(I32), w_dram[1])
         nc.sync.dma_start(f_right[:], frac)
         nc.sync.dma_start(right_sb[:], right)
         nc.sync.dma_start(left_sb[:], left)
@@ -115,7 +118,7 @@ def tile_picked_lerp_none_e_kernel(tc, xT, w1_words, w1_scales, frac, offs, left
             cols = slice(m * P, (m + 1) * P)
             nc.tensor.matmul_mx(
                 out=banks[grp][:],
-                lhsT=w_words[g][:, cols].bitcast(FP8X4),
+                lhsT=w_words[g][m].bitcast(FP8X4),
                 lhsT_scale=w_scales[:, g, cols],
                 rhs=codes[g][:, a:b].bitcast(FP8X4),
                 rhs_scale=scales[g][:, a:b],
@@ -129,23 +132,23 @@ def tile_picked_lerp_none_e_kernel(tc, xT, w1_words, w1_scales, frac, offs, left
 
         gather_into_place(7, 0, SLICE)
         gather_into_place(7, SLICE, HALF)
-        gather(on_s, 7, HALF, HALF + SLICE)
-        gather(on_s, 7, HALF + SLICE, S)
-        nc.gpsimd.tensor_scalar(*pair_views(3, HALF, HALF + SLICE), 1.0, 0.0, MULT, ADD)
-        nc.scalar.activation(*pair_views(3, HALF + SLICE, S), COPY)
+        cuts = (HALF, 320, 416, S)
+        for a, b in zip(cuts, cuts[1:]):
+            gather(on_s, 7, a, b)
+        nc.gpsimd.tensor_scalar(*pair_views(3, cuts[0], cuts[1]), 1.0, 0.0, MULT, ADD)
+        for a, b in zip(cuts[1:], cuts[2:]):
+            nc.scalar.activation(*pair_views(3, a, b), COPY)
         for i in range(4):
             quantize(1, i * SLICE, (i + 1) * SLICE)
 
-        for grp in groups[:7]:
+        for grp in groups:
             product(0, grp)
         product(1, groups[0])
         product(1, groups[4])
         for grp in groups[1:4]:
             product(1, grp)
-        product(1, groups[5])
-        product(0, groups[7])
-        product(1, groups[6])
-        product(1, groups[7])
+        for grp in groups[5:]:
+            product(1, grp)
 
         empty(nc.scalar.copy, groups[0])
         empty(nc.vector.tensor_copy, groups[4])
@@ -154,7 +157,7 @@ def tile_picked_lerp_none_e_kernel(tc, xT, w1_words, w1_scales, frac, offs, left
         f_left = sb.tile([P, V], F32, name="f_left", tag="woven1", align_bytes=64)
         nc.vector.tensor_scalar(f_left[:], f_right[:], -1.0, 1.0, MULT, ADD)
         empty(nc.vector.tensor_copy, groups[5])
-        empty(nc.scalar.copy, groups[6])
+        empty(nc.vector.tensor_copy, groups[6])
         empty(nc.scalar.copy, groups[7])
 
         lo = [sb.tile([P, V], F32, name="lo%d" % m) for m in range(2)]

@@ -143,12 +143,12 @@ def tile_picked_lerp_none_e_kernel(tc, xT, w1_words, w1_scales, frac, offs, left
 
         for grp in groups:
             product(0, grp)
-        product(1, groups[0])
-        product(1, groups[4])
-        for grp in groups[1:4]:
-            product(1, grp)
-        for grp in groups[5:]:
-            product(1, grp)
+        for i in range(2):
+            for m in range(2):
+                product(1, groups[4 * m + i])
+        for m in range(2):
+            for i in range(2, 4):
+                product(1, groups[4 * m + i])
 
         empty(nc.scalar.copy, groups[0])
         empty(nc.vector.tensor_copy, groups[4])

@@ -35,24 +35,23 @@ def tile_picked_lerp_none_e_kernel(tc, xT, w1_words, w1_scales, frac, offs, left
 
         x_rows = xT.rearrange("(g p j) t -> g j p t", g=PASSES, j=4)
         rows = [sb.tile([P, T], F32, name="row%d" % r, align_bytes=64) for r in range(8)]
+        scales = [sb.tile([P, S], U8, name="scales%d" % g, align_bytes=64) for g in range(PASSES)]
         nc.sync.dma_start(rows[0][:], x_rows[0, 0])
         nc.sync.dma_start(offs_sb[:], offs)
-        for r in range(1, 7):
+        for r in range(1, 8):
             nc.sync.dma_start(rows[r][:], x_rows[r // 4, r % 4])
+            if r <= 4:
+                q = r - 1
+                nc.sync.dma_start(
+                    scales[0][32 * q + 4 : 32 * q + 8, :].bitcast(I32).rearrange("r (g n) -> r g n", g=PASSES),
+                    w1_scales[:, 4 * q : 4 * q + 4, :].rearrange("g r n -> r g n").bitcast(I32),
+                )
 
         first_words = [sb.tile([P, P], U32, name="first_words%d" % m, align_bytes=64) for m in range(2)]
         last_words = sb.tile([P, N], U32, name="last_words", align_bytes=64)
         w_words = [[first_words[0][:], first_words[1][:]], [last_words[:, 0:P], last_words[:, P:N]]]
-        w_scales = sb.tile([P, PASSES, N], U8, name="w_scales", align_bytes=64)
         f_right = sb.tile([P, V], F32, name="f_right")
-        nc.gpsimd.memset(w_scales[:].rearrange("p g n -> p (g n)").bitcast(I32), 0)
-        for q in range(4):
-            nc.sync.dma_start(
-                w_scales[32 * q : 32 * q + 4, :, :].bitcast(I32),
-                w1_scales[:, 4 * q : 4 * q + 4, :].rearrange("g r n -> r g n").bitcast(I32),
-            )
         w_dram = w1_words.rearrange("g p n t -> g p (n t)").bitcast(I32)
-        nc.sync.dma_start(rows[7][:], x_rows[1, 3])
         for m in range(2):
             nc.sync.dma_start(first_words[m][:].bitcast(I32), w_dram[0][:, m * P : (m + 1) * P])
         nc.sync.dma_start(last_words[:].bitcast(I32), w_dram[1])
@@ -63,7 +62,6 @@ def tile_picked_lerp_none_e_kernel(tc, xT, w1_words, w1_scales, frac, offs, left
         picked = [sb.tile([P, 2, S], F32, name="picked%d" % u, align_bytes=64) for u in range(4)]
         woven = [sb.tile([P, 4 * S], BF16, name="woven%d" % g, tag="woven%d" % g, align_bytes=64) for g in range(PASSES)]
         codes = [sb.tile([P, S], U32, name="codes%d" % g, align_bytes=64) for g in range(PASSES)]
-        scales = [sb.tile([P, S], U8, name="scales%d" % g, align_bytes=64) for g in range(PASSES)]
 
         def on_s(dst, window, offsets):
             nc.scalar.activation(dst, window.indirect(offsets), COPY)
@@ -115,11 +113,11 @@ def tile_picked_lerp_none_e_kernel(tc, xT, w1_words, w1_scales, frac, offs, left
 
         def product(g, grp):
             m, a, b = grp
-            cols = slice(m * P, (m + 1) * P)
+            cols = slice(g * N + m * P, g * N + (m + 1) * P)
             nc.tensor.matmul_mx(
                 out=banks[grp][:],
                 lhsT=w_words[g][m].bitcast(FP8X4),
-                lhsT_scale=w_scales[:, g, cols],
+                lhsT_scale=scales[0][4:P, cols],
                 rhs=codes[g][:, a:b].bitcast(FP8X4),
                 rhs_scale=scales[g][:, a:b],
                 start=(g == 0),

@@ -33,19 +33,31 @@ def tile_picked_lerp_none_e_kernel(tc, xT, w1_words, w1_scales, frac, offs, left
         left_sb = lists.tile([P, V // 16], U16, name="left_sb")
         right_sb = lists.tile([P, V // 16], U16, name="right_sb")
 
-        x_rows = xT.rearrange("(g p j) t -> g j p t", g=PASSES, j=4)
-        rows = [sb.tile([P, T], F32, name="row%d" % r, align_bytes=64) for r in range(8)]
+        warm = sb.tile([P, 2], F32, name="warm")
+        nc.gpsimd.memset(warm[:, 0:1], 0.0)
+        nc.scalar.activation(warm[:, 1:2], warm[:, 0:1], COPY)
+
+        x_rows = xT.rearrange("(g p j) t -> g p j t", g=PASSES, j=4)
+        pairs = [sb.tile([P, 2, T], F32, name="pair%d" % u, align_bytes=64) for u in range(2)]
+        singles = [sb.tile([P, T], F32, name="row%d" % r, align_bytes=64) for r in range(4, 8)]
+        rows = [pairs[r // 2][:, r % 2, :] for r in range(4)] + [row[:] for row in singles]
         scales = [sb.tile([P, S], U8, name="scales%d" % g, align_bytes=64) for g in range(PASSES)]
-        nc.sync.dma_start(rows[0][:], x_rows[0, 0])
+        def load_scales(q):
+            nc.sync.dma_start(
+                scales[0][32 * q + 4 : 32 * q + 8, :].bitcast(I32).rearrange("r (g n) -> r g n", g=PASSES),
+                w1_scales[:, 4 * q : 4 * q + 4, :].rearrange("g r n -> r g n").bitcast(I32),
+            )
+
+        nc.sync.dma_start(pairs[0][:], x_rows[0, :, 0:2, :])
         nc.sync.dma_start(offs_sb[:], offs)
-        for r in range(1, 8):
-            nc.sync.dma_start(rows[r][:], x_rows[r // 4, r % 4])
-            if r <= 4:
-                q = r - 1
-                nc.sync.dma_start(
-                    scales[0][32 * q + 4 : 32 * q + 8, :].bitcast(I32).rearrange("r (g n) -> r g n", g=PASSES),
-                    w1_scales[:, 4 * q : 4 * q + 4, :].rearrange("g r n -> r g n").bitcast(I32),
-                )
+        load_scales(0)
+        nc.sync.dma_start(pairs[1][:], x_rows[0, :, 2:4, :])
+        load_scales(1)
+        load_scales(2)
+        nc.sync.dma_start(rows[4], x_rows[1, :, 0, :])
+        load_scales(3)
+        for r in range(5, 8):
+            nc.sync.dma_start(rows[r], x_rows[1, :, r % 4, :])
 
         first_words = [sb.tile([P, P], U32, name="first_words%d" % m, align_bytes=64) for m in range(2)]
         last_words = sb.tile([P, N], U32, name="last_words", align_bytes=64)
@@ -70,10 +82,10 @@ def tile_picked_lerp_none_e_kernel(tc, xT, w1_words, w1_scales, frac, offs, left
             nc.vector.tensor_copy(dst, window.indirect(offsets))
 
         def gather(engine, r, a, b):
-            engine(picked[r // 2][:, r % 2, a:b], rows[r][:], offs_sb[:, a // 16 : b // 16])
+            engine(picked[r // 2][:, r % 2, a:b], rows[r], offs_sb[:, a // 16 : b // 16])
 
         def gather_into_place(r, a, b):
-            on_v(woven[r // 4][:].rearrange("p (s j) -> p j s", j=4)[:, r % 4, a:b], rows[r][:], offs_sb[:, a // 16 : b // 16])
+            on_v(woven[r // 4][:].rearrange("p (s j) -> p j s", j=4)[:, r % 4, a:b], rows[r], offs_sb[:, a // 16 : b // 16])
 
         def pair_views(u, a, b):
             return (
@@ -87,20 +99,17 @@ def tile_picked_lerp_none_e_kernel(tc, xT, w1_words, w1_scales, frac, offs, left
         def quantize(g, a, b):
             nc.vector.quantize_mx(out=codes[g][:, a:b].bitcast(FP8X4), scales=scales[g][:, a:b], in_=woven[g][:, 4 * a : 4 * b])
 
-        gather(on_v, 0, 0, 448)
-        gather(on_s, 0, 448, S)
-        gather(on_v, 1, 0, S)
-        place(0, 0, S)
-        gather(on_s, 2, 0, S)
-        gather(on_v, 3, 0, HALF)
-        gather(on_s, 3, HALF, S)
-        place(1, HALF, S)
-        place(1, 0, HALF)
-        quantize(0, HALF, S)
-        quantize(0, 0, HALF)
-        gather(on_s, 4, 0, S)
-        gather(on_v, 5, 0, SLICE)
-        gather(on_s, 5, SLICE, HALF)
+        for u in range(2):
+            for a in (HALF, 0):
+                gather(on_v, 2 * u, a, a + HALF)
+                gather(on_s, 2 * u + 1, a, a + HALF)
+            for a in (HALF, 0):
+                place(u, a, a + HALF)
+        for a in (HALF, 0):
+            quantize(0, a, a + HALF)
+        gather(on_v, 4, 0, SLICE)
+        gather(on_s, 4, SLICE, S)
+        gather(on_s, 5, 0, HALF)
         gather(on_s, 5, HALF, S)
         place(2, 0, HALF)
         nc.gpsimd.tensor_scalar(*pair_views(2, HALF, S), 1.0, 0.0, MULT, ADD)

from contextlib import ExitStack

import concourse.mybir as mybir

K, T, S, V, N = 1024, 1024, 512, 256, 256
FLOPS = 2 * K * S * N

F32 = mybir.dt.float32
BF16 = mybir.dt.bfloat16
I32 = mybir.dt.int32
U32 = mybir.dt.uint32
U16 = mybir.dt.uint16
U8 = mybir.dt.uint8
FP8X4 = mybir.dt.float8_e4m3fn_x4
MULT = mybir.AluOpType.mult
ADD = mybir.AluOpType.add
COPY = mybir.ActivationFunctionType.Copy

P = 128
PASSES = 2
SLICE = 128
HALF = 256


def tile_picked_lerp_none_e_kernel(tc, xT, w1_words, w1_scales, frac, offs, left, right, out):
    nc = tc.nc
    with ExitStack() as ctx:
        lists = ctx.enter_context(tc.tile_pool(name="lists", bufs=1))
        sb = ctx.enter_context(tc.tile_pool(name="sb", bufs=1))
        psum = ctx.enter_context(tc.psum_pool(name="psum", bufs=1))

        offs_sb = lists.tile([P, S // 16], U16, name="offs_sb")
        left_sb = lists.tile([P, V // 16], U16, name="left_sb")
        right_sb = lists.tile([P, V // 16], U16, name="right_sb")

        warm = sb.tile([P, 2], F32, name="warm")
        nc.gpsimd.memset(warm[:, 0:1], 0.0)
        nc.scalar.activation(warm[:, 1:2], warm[:, 0:1], COPY)

        x_rows = xT.rearrange("(g p j) t -> g p j t", g=PASSES, j=4)
        pairs = [sb.tile([P, 2, T], F32, name="pair%d" % u, align_bytes=64) for u in range(2)]
        singles = [sb.tile([P, T], F32, name="row%d" % r, align_bytes=64) for r in range(4, 8)]
        rows = [pairs[r // 2][:, r % 2, :] for r in range(4)] + [row[:] for row in singles]
        scales = [sb.tile([P, S], U8, name="scales%d" % g, align_bytes=64) for g in range(PASSES)]
        def load_scales(q):
            nc.sync.dma_start(
                scales[0][32 * q + 4 : 32 * q + 8, :].bitcast(I32).rearrange("r (g n) -> r g n", g=PASSES),
                w1_scales[:, 4 * q : 4 * q + 4, :].rearrange("g r n -> r g n").bitcast(I32),
            )

        nc.sync.dma_start(pairs[0][:], x_rows[0, :, 0:2, :])
        nc.sync.dma_start(offs_sb[:], offs)
        load_scales(0)
        nc.sync.dma_start(pairs[1][:], x_rows[0, :, 2:4, :])
        load_scales(1)
        load_scales(2)
        nc.sync.dma_start(rows[4], x_rows[1, :, 0, :])
        load_scales(3)
        for r in range(5, 8):
            nc.sync.dma_start(rows[r], x_rows[1, :, r % 4, :])

        first_words = [sb.tile([P, P], U32, name="first_words%d" % m, align_bytes=64) for m in range(2)]
        last_words = sb.tile([P, N], U32, name="last_words", align_bytes=64)
        w_words = [[first_words[0][:], first_words[1][:]], [last_words[:, 0:P], last_words[:, P:N]]]
        f_right = sb.tile([P, V], F32, name="f_right")
        w_dram = w1_words.rearrange("g p n t -> g p (n t)").bitcast(I32)
        for m in range(2):
            nc.sync.dma_start(first_words[m][:].bitcast(I32), w_dram[0][:, m * P : (m + 1) * P])
        nc.sync.dma_start(last_words[:].bitcast(I32), w_dram[1])
        nc.sync.dma_start(f_right[:], frac)
        nc.sync.dma_start(right_sb[:], right)
        nc.sync.dma_start(left_sb[:], left)

        picked = [sb.tile([P, 2, S], F32, name="picked%d" % u, align_bytes=64) for u in range(4)]
        woven = [sb.tile([P, 4 * S], BF16, name="woven%d" % g, tag="woven%d" % g, align_bytes=64) for g in range(PASSES)]
        codes = [sb.tile([P, S], U32, name="codes%d" % g, align_bytes=64) for g in range(PASSES)]

        def on_s(dst, window, offsets):
            nc.scalar.activation(dst, window.indirect(offsets), COPY)

        def on_v(dst, window, offsets):
            nc.vector.tensor_copy(dst, window.indirect(offsets))

        def gather(engine, r, a, b):
            engine(picked[r // 2][:, r % 2, a:b], rows[r], offs_sb[:, a // 16 : b // 16])

        def gather_into_place(r, a, b):
            on_v(woven[r // 4][:].rearrange("p (s j) -> p j s", j=4)[:, r % 4, a:b], rows[r], offs_sb[:, a // 16 : b // 16])

        def pair_views(u, a, b):
            return (
                woven[u // 2][:].rearrange("p (s j) -> p s j", j=4)[:, a:b, 2 * (u % 2) : 2 * (u % 2) + 2],
                picked[u][:].rearrange("p e s -> p s e")[:, a:b, :],
            )

        def place(u, a, b):
            nc.vector.tensor_copy(*pair_views(u, a, b))

        def quantize(g, a, b):
            nc.vector.quantize_mx(out=codes[g][:, a:b].bitcast(FP8X4), scales=scales[g][:, a:b], in_=woven[g][:, 4 * a : 4 * b])

        for u in range(2):
            for a in (HALF, 0):
                gather(on_v, 2 * u, a, a + HALF)
                gather(on_s, 2 * u + 1, a, a + HALF)
            for a in (HALF, 0):
                place(u, a, a + HALF)
        for a in (HALF, 0):
            quantize(0, a, a + HALF)
        gather(on_v, 4, 0, SLICE)
        gather(on_s, 4, SLICE, S)
        gather(on_s, 5, 0, HALF)
        gather(on_s, 5, HALF, S)
        place(2, 0, HALF)
        nc.gpsimd.tensor_scalar(*pair_views(2, HALF, S), 1.0, 0.0, MULT, ADD)
        gather_into_place(6, 0, HALF)
        gather(on_s, 6, HALF, S)

        groups = [(m, i * SLICE, (i + 1) * SLICE) for m in range(2) for i in range(4)]
        banks = {grp: psum.tile([P, grp[2] - grp[1]], F32, name="bank%d_%d" % grp[:2]) for grp in groups}
        y = [sb.tile([P, S], F32, name="y%d" % m, tag="y%d" % m) for m in range(2)]

        def product(g, grp):
            m, a, b = grp
            cols = slice(g * N + m * P, g * N + (m + 1) * P)
            nc.tensor.matmul_mx(
                out=banks[grp][:],
                lhsT=w_words[g][m].bitcast(FP8X4),
                lhsT_scale=scales[0][4:P, cols],
                rhs=codes[g][:, a:b].bitcast(FP8X4),
                rhs_scale=scales[g][:, a:b],
                start=(g == 0),
                stop=(g == PASSES - 1),
            )

        def empty(copy, grp):
            m, a, b = grp
            copy(y[m][:, a:b], banks[grp][:])

        gather_into_place(7, 0, SLICE)
        gather_into_place(7, SLICE, HALF)
        cuts = (HALF, 320, 416, S)
        for a, b in zip(cuts, cuts[1:]):
            gather(on_s, 7, a, b)
        nc.gpsimd.tensor_scalar(*pair_views(3, cuts[0], cuts[1]), 1.0, 0.0, MULT, ADD)
        for a, b in zip(cuts[1:], cuts[2:]):
            nc.scalar.activation(*pair_views(3, a, b), COPY)
        for i in range(4):
            quantize(1, i * SLICE, (i + 1) * SLICE)

        for grp in groups:
            product(0, grp)
        for i in range(2):
            for m in range(2):
                product(1, groups[4 * m + i])
        for m in range(2):
            for i in range(2, 4):
                product(1, groups[4 * m + i])

        empty(nc.scalar.copy, groups[0])
        empty(nc.vector.tensor_copy, groups[4])
        for grp in groups[1:4]:
            empty(nc.scalar.copy, grp)
        f_left = sb.tile([P, V], F32, name="f_left", tag="woven1", align_bytes=64)
        nc.vector.tensor_scalar(f_left[:], f_right[:], -1.0, 1.0, MULT, ADD)
        empty(nc.vector.tensor_copy, groups[5])
        empty(nc.vector.tensor_copy, groups[6])
        empty(nc.scalar.copy, groups[7])

        lo = [sb.tile([P, V], F32, name="lo%d" % m) for m in range(2)]
        hi = [sb.tile([P, V], F32, name="hi%d" % m) for m in range(2)]
        at_left = [sb.tile([P, V], F32, name="at_left%d" % m) for m in range(2)]
        res = [sb.tile([P, V], F32, name="res%d" % m) for m in range(2)]
        for m in range(2):
            on_s(at_left[m][:], y[m][:], left_sb[:])
            nc.vector.tensor_tensor(hi[m][:], y[m][:].indirect(right_sb[:]), f_right[:], MULT)
        for m in range(2):
            nc.vector.tensor_tensor(lo[m][:], at_left[m][:], f_left[:], MULT)
        for m in range(2):
            nc.vector.tensor_tensor(res[m][:], lo[m][:], hi[m][:], ADD)
            nc.sync.dma_start(out[m * P : (m + 1) * P, :], res[m][:])
